import numpy as np
import ml_dtypes


def mxq(x, axis, fmt="e4m3"):
    dtype, down = {"e4m3": (ml_dtypes.float8_e4m3fn, 7), "e5m2": (ml_dtypes.float8_e5m2, 14)}[fmt]
    v = np.moveaxis(np.asarray(x, np.float32).astype(ml_dtypes.bfloat16).astype(np.float64), axis, -1)
    blocks = v.reshape(v.shape[:-1] + (-1, 32))
    amax = np.abs(blocks).max(-1, keepdims=True)
    byte = np.maximum(np.where(amax > 0, np.frexp(amax)[1] - 1 + 127, 0) - down, 1)
    scale = np.exp2(byte - 127.0)
    codes = (blocks / scale).astype(np.float32).astype(dtype).astype(np.float64)
    return np.moveaxis((codes * scale).reshape(v.shape), -1, axis)


WIDE = False


def mx_kscale(k):
    if not WIDE:
        return np.ones(k)
    levels = np.array([18, -18])
    if k % 512:
        return np.exp2(np.random.permutation(np.resize(levels, k // 32))).repeat(32)
    a = np.empty((k // 512, 16))
    for p in range(k // 512):
        a[p, :8] = np.random.permutation(np.resize(levels, 8))
        for g in range(8):
            far = levels[np.abs(levels - a[p, g]) >= 10]
            a[p, g + 8] = far[np.random.randint(len(far))]
    return np.exp2(a.ravel()).repeat(32)


def f64(x):
    return np.asarray(x).astype(np.float64)


def striped(idx):
    return np.tile(np.asarray(idx).reshape(-1, 16).T, (8, 1)).astype(np.uint16)


def unstriped(offs):
    return offs[:16].T.reshape(-1).astype(np.int64)


E2M1 = np.array([0.0, 0.5, 1.0, 1.5, 2.0, 3.0, 4.0, 6.0, -0.0, -0.5, -1.0, -1.5, -2.0, -3.0, -4.0, -6.0])


def pack_weight(w, fmt):
    k, n = w.shape
    w = f64(np.asarray(w, np.float32).astype(ml_dtypes.bfloat16)).reshape(k // 32, 32, n)
    amax = np.abs(w).max(1)
    if fmt == "e4m3":
        byte = np.frexp(amax)[1] - 1 + 127 - 7
    else:
        mant, ex = np.frexp(amax / 6.0)
        byte = np.where(mant > 0.5, ex, ex - 1) + 127
    byte = np.clip(np.where(amax > 0, byte, 1), 1, 254)
    scaled = (w * np.exp2(127.0 - byte)[:, None, :]).reshape(k, n).astype(np.float32)
    by_word = np.ascontiguousarray(scaled.reshape(k // 512, 128, 4, n).transpose(0, 1, 3, 2))
    if fmt == "e4m3":
        words = by_word.astype(ml_dtypes.float8_e4m3fn).view(np.uint8)
    else:
        c = by_word.astype(ml_dtypes.float4_e2m1fn).view(np.uint8) & 0xF
        words = (c[..., 0::2] | (c[..., 1::2] << 4)).reshape(k // 512, 128, 2 * n)
    return np.ascontiguousarray(words), np.ascontiguousarray(byte.astype(np.uint8).reshape(k // 512, 16, n))


def unpack_weight(words, scales, fmt):
    g, _, n = scales.shape
    words = np.ascontiguousarray(words).reshape(g, 128, n, -1)
    if fmt == "e4m3":
        vals = words.view(ml_dtypes.float8_e4m3fn).astype(np.float64)
    else:
        nib = np.empty((g, 128, n, 4), np.uint8)
        nib[..., 0::2] = words & 0xF
        nib[..., 1::2] = words >> 4
        vals = E2M1[nib]
    vals = vals * np.repeat(np.exp2(scales.astype(np.float64) - 127.0), 8, axis=1)[..., None]
    return vals.transpose(0, 1, 3, 2).reshape(g * 512, n)


B, N, T, D, R = 1, 512, 2048, 1024, 512


def setup_inputs():
    n = np.random.standard_normal
    idx = np.random.permutation(T)[:B * N]
    s = mx_kscale(D)[:, None]
    z = mx_kscale(R)[:, None]
    x = n((B, D, R))
    wp = pack_weight(n((D, T)) * (1.00 / np.sqrt(D)) / s, "e2m1")
    return {
        "xT": (x * s).astype(np.float32),
        "w_words": np.ascontiguousarray(wp[0].reshape(1, 2, 128, T, 2).transpose(0, 2, 3, 1, 4)).reshape(1, 128, T, 4),
        "w_scales": wp[1],
        "y": n((B, R, N)).astype(np.float32),
        "wt": (np.random.uniform(0.5, 1.5, (B, R, 1)) * 1.0 / np.sqrt(R) * z).astype(np.float32),
        "xm": (x.transpose(0, 2, 1) / z).astype(np.float32),
        "offs": striped(idx),
    }


def reference(xT, w_words, w_scales, y, wt, xm, offs):
    idx = unstriped(offs)
    w = unpack_weight(w_words.reshape(1, 128, T, 2, 2).transpose(0, 3, 1, 2, 4).reshape(2, 128, 2 * T), w_scales, "e2m1")
    pick = lambda x: x[:, idx].reshape(x.shape[0], B, N).transpose(1, 0, 2)
    a = mxq(f64(xT), 1, "e4m3").transpose(0, 2, 1) @ pick(w)
    g = f64(wt) * (a - f64(y))
    dw = mxq(f64(xm), 1, "e4m3").transpose(0, 2, 1) @ mxq(g, 1, "e5m2")
    gw = np.zeros((D, T))
    gw[:, idx] = dw.transpose(1, 0, 2).reshape(D, B * N)
    return gw

@@ -1,0 +1,176 @@
+from contextlib import ExitStack
+
+import concourse.mybir as mybir
+
+D, T, R, N = 1024, 2048, 512, 512
+FLOPS = 2 * 2 * R * N * D
+
+F32 = mybir.dt.float32
+BF16 = mybir.dt.bfloat16
+I32 = mybir.dt.int32
+U32 = mybir.dt.uint32
+U16 = mybir.dt.uint16
+U8 = mybir.dt.uint8
+E4M3 = mybir.dt.float8_e4m3fn_x4
+E5M2 = mybir.dt.float8_e5m2_x4
+E2M1 = mybir.dt.float4_e2m1fn_x4
+COPY = mybir.ActivationFunctionType.Copy
+MULT = mybir.AluOpType.mult
+SUB = mybir.AluOpType.subtract
+
+P = 128
+PACK = 4
+PASSES = D // (P * PACK)
+BLOCKS = D // P
+XM_CHUNK = 256
+WINDOWS = 3
+VECTOR_M = (40, 84)
+HALF = N // 2
+
+
+def tile_attend_gsq_w_kernel(tc, xT, w_words, w_scales, y, wt, xm, offs, out):
+    nc = tc.nc
+    with ExitStack() as ctx:
+        keep = ctx.enter_context(tc.tile_pool(name="keep", bufs=1))
+        ring = ctx.enter_context(tc.tile_pool(name="ring", bufs=3))
+        psum_a = ctx.enter_context(tc.psum_pool(name="psum_a", bufs=1))
+        psum_dw = ctx.enter_context(tc.psum_pool(name="psum_dw", bufs=4))
+
+        offsets = keep.tile([P, N // 16], U16, name="offsets")
+        word_table = keep.tile([P, T], I32, name="word_table", align_bytes=64)
+        scale_table = keep.tile([P, PASSES, T], U8, name="scale_table", align_bytes=64)
+        weights = keep.tile([P, PACK], F32, name="weights")
+        xt_raw = [keep.tile([P, PACK, R], F32, name="xt_raw%d" % o, align_bytes=64) for o in range(PASSES)]
+        y_raw = keep.tile([P, PACK, N], F32, name="y_raw", align_bytes=64)
+        xm_raw = [keep.tile([P, PACK, XM_CHUNK], F32, name="xm_raw%d" % c, align_bytes=64) for c in range(D // XM_CHUNK)]
+        windows = [keep.tile([P, T], F32, name="window%d" % w, align_bytes=64) for w in range(WINDOWS)]
+
+        nc.vector.memset(scale_table[:].rearrange("p o t -> p (o t)").bitcast(I32), 0)
+
+        nc.sync.dma_start(word_table[:], w_words[0].rearrange("p t b -> p (t b)").bitcast(I32))
+        nc.sync.dma_start(offsets[:], offs)
+        for q in range(4):
+            nc.sync.dma_start(
+                scale_table[32 * q : 32 * q + 4, :, :].bitcast(I32),
+                w_scales[:, 4 * q : 4 * q + 4, :].rearrange("o f t -> f o t").bitcast(I32),
+            )
+        for o in range(PASSES):
+            nc.sync.dma_start(xt_raw[o][:], xT[0, 512 * o : 512 * (o + 1), :].rearrange("(p j) r -> p j r", j=PACK))
+        nc.sync.dma_start(weights[:], wt[0].rearrange("(p t) one -> p (t one)", t=PACK))
+        nc.sync.dma_start(y_raw[:], y[0].rearrange("(p t) i -> p t i", t=PACK))
+        xm_rows = xm[0].rearrange("(p t) d -> p t d", t=PACK)
+        for c in range(D // XM_CHUNK):
+            nc.sync.dma_start(xm_raw[c][:], xm_rows[:, :, c * XM_CHUNK : (c + 1) * XM_CHUNK])
+
+        for w in range(WINDOWS):
+            nc.vector.memset(windows[w][:], 0.0)
+
+        pair_words = keep.tile([P, N], U32, name="pair_words", align_bytes=64)
+        nc.vector.tensor_copy(pair_words[:], word_table[:].bitcast(U32).indirect(offsets[:]))
+        w_scale = keep.tile([P, PASSES, N], U8, name="w_scale", align_bytes=64)
+        nc.vector.tensor_copy(w_scale[:, 0, :], scale_table[:, 0, :].indirect(offsets[:]))
+        w_codes = keep.tile([P, PASSES, 2 * N], U8, name="w_codes", align_bytes=64)
+        halves = pair_words[:].bitcast(U16).rearrange("p (i o) -> p o i", o=PASSES)
+        for o in range(PASSES):
+            nc.vector.tensor_copy(w_codes[:, o, :].bitcast(U16), halves[:, o, :])
+        nc.vector.tensor_copy(w_scale[:, 1, :], scale_table[:, 1, :].indirect(offsets[:]))
+
+        xt_bf = [keep.tile([P, PACK, P, PACK], BF16, name="xt_bf%d" % o, align_bytes=64) for o in range(PASSES)]
+        xt_codes = keep.tile([P, PASSES, R], U32, name="xt_codes", align_bytes=64)
+        xt_scale = keep.tile([P, PASSES, R], U8, name="xt_scale", align_bytes=64)
+        banks = [psum_a.tile([P, N], F32, name="a%d" % t) for t in range(PACK)]
+        for o in range(PASSES):
+            src = xt_raw[o][:].rearrange("p j (m t) -> p m j t", t=PACK)
+            dst = xt_bf[o][:].rearrange("p t m j -> p m j t")
+            mv = VECTOR_M[o]
+            nc.scalar.copy(dst[:, mv:, :, :], src[:, mv:, :, :])
+            nc.vector.tensor_copy(dst[:, :mv, :, :], src[:, :mv, :, :])
+            for h in range(2):
+                nc.vector.quantize_mx(
+                    out=xt_codes[:, o, 256 * h : 256 * (h + 1)].bitcast(E4M3),
+                    scales=xt_scale[:, o, 256 * h : 256 * (h + 1)],
+                    in_=xt_bf[o][:, 2 * h : 2 * h + 2, :, :].rearrange("p t m j -> p (t m j)"),
+                )
+            for t in range(PACK):
+                nc.tensor.matmul_mx(
+                    out=banks[t][:],
+                    lhsT=xt_codes[:, o, P * t : P * (t + 1)].bitcast(E4M3),
+                    lhsT_scale=xt_scale[:, o, P * t : P * (t + 1)],
+                    rhs=w_codes[:, o, :].bitcast(E2M1),
+                    rhs_scale=w_scale[:, o, :],
+                    start=(o == 0),
+                    stop=(o == PASSES - 1),
+                )
+
+        aw = [keep.tile([P, PACK, HALF], F32, name="aw%d" % h, align_bytes=64) for h in range(2)]
+        yw = keep.tile([P, PACK, N], F32, name="yw", align_bytes=64)
+        g_bf = keep.tile([P, N, PACK], BF16, name="g_bf", align_bytes=64)
+        g_codes = keep.tile([P, N], U32, name="g_codes", align_bytes=64)
+        g_scale = keep.tile([P, N], U8, name="g_scale", align_bytes=64)
+        for t in range(PACK):
+            nc.vector.tensor_scalar(yw[:, t, :], y_raw[:, t, :], weights[:, t : t + 1], None, MULT)
+        for h in range(2):
+            cols = slice(h * HALF, (h + 1) * HALF)
+            for t in range(PACK):
+                nc.scalar.activation(aw[h][:, t, :], banks[t][:, cols], COPY, scale=weights[:, t : t + 1])
+        for h in range(2):
+            cols = slice(h * HALF, (h + 1) * HALF)
+            nc.vector.tensor_tensor(
+                g_bf[:, cols, :].rearrange("p (c i) t -> p c t i", i=4),
+                aw[h][:].rearrange("p t (c i) -> p c t i", i=4),
+                yw[:, :, cols].rearrange("p t (c i) -> p c t i", i=4),
+                SUB,
+            )
+        for h in range(2):
+            cols = slice(h * HALF, (h + 1) * HALF)
+            nc.vector.quantize_mx(
+                out=g_codes[:, cols].bitcast(E5M2),
+                scales=g_scale[:, cols],
+                in_=g_bf[:, cols, :].rearrange("p i t -> p (i t)"),
+            )
+
+        xm_bf = [keep.tile([P, P, PACK], BF16, name="xm_bf%d" % b, align_bytes=64) for b in range(BLOCKS)]
+        xm_codes = [keep.tile([P, P], U32, name="xm_codes%d" % b, align_bytes=64) for b in range(BLOCKS)]
+        xm_scale = [keep.tile([P, P], U8, name="xm_scale%d" % b, align_bytes=64) for b in range(BLOCKS)]
+
+        def prepare(b):
+            c, lo = divmod(b * P, XM_CHUNK)
+            nc.scalar.copy(
+                xm_bf[b][:].rearrange("p (c i) t -> p c t i", i=4),
+                xm_raw[c][:, :, lo : lo + P].rearrange("p t (c i) -> p c t i", i=4),
+            )
+            nc.vector.quantize_mx(
+                out=xm_codes[b][:].bitcast(E4M3),
+                scales=xm_scale[b][:],
+                in_=xm_bf[b][:].rearrange("p d t -> p (d t)"),
+            )
+
+        def multiply(b):
+            acc = psum_dw.tile([P, N], F32, name="acc")
+            nc.tensor.matmul_mx(
+                out=acc[:],
+                lhsT=xm_codes[b][:].bitcast(E4M3),
+                lhsT_scale=xm_scale[b][:],
+                rhs=g_codes[:].bitcast(E5M2),
+                rhs_scale=g_scale[:],
+                start=True,
+                stop=True,
+            )
+            dense = ring.tile([P, N], F32, name="dense", align_bytes=64)
+            nc.scalar.copy(dense[:], acc[:])
+            return dense
+
+        def place(b, dense):
+            window = windows[b % WINDOWS]
+            nc.vector.tensor_copy(window[:].indirect(offsets[:]), dense[:])
+            nc.sync.dma_start(out[b * P : (b + 1) * P, :], window[:])
+
+        prepare(0)
+        dense = multiply(0)
+        prepare(1)
+        for b in range(BLOCKS):
+            following = multiply(b + 1) if b + 1 < BLOCKS else None
+            place(b, dense)
+            if b + 2 < BLOCKS:
+                prepare(b + 2)
+            dense = following

@@ -22,7 +22,8 @@ P = 128
 PACK = 4
 PASSES = D // (P * PACK)
 BLOCKS = D // P
-XM_CHUNK = 256
+XM_CHUNKS = ((0, 256), (256, 512), (512, 1024))
+XM_GROUPS = ((0, 1), (1, 2), (2, 4), (4, 6), (6, 8))
 WINDOWS = 3
 VECTOR_M = (40, 84)
 HALF = N // 2
@@ -41,14 +42,15 @@ def tile_attend_gsq_w_kernel(tc, xT, w_words, w_scales, y, wt, xm, offs, out):
         scale_table = keep.tile([P, PASSES, T], U8, name="scale_table", align_bytes=64)
         weights = keep.tile([P, PACK], F32, name="weights")
         xt_raw = [keep.tile([P, PACK, R], F32, name="xt_raw%d" % o, align_bytes=64) for o in range(PASSES)]
-        y_raw = keep.tile([P, PACK, N], F32, name="y_raw", align_bytes=64)
-        xm_raw = [keep.tile([P, PACK, XM_CHUNK], F32, name="xm_raw%d" % c, align_bytes=64) for c in range(D // XM_CHUNK)]
+        y_raw = [keep.tile([P, 2, N], F32, name="y_raw%d" % u, align_bytes=64) for u in range(2)]
+        xm_raw = [keep.tile([P, PACK, hi - lo], F32, name="xm_raw%d" % lo, align_bytes=64) for lo, hi in XM_CHUNKS]
         windows = [keep.tile([P, T], F32, name="window%d" % w, align_bytes=64) for w in range(WINDOWS)]
 
         nc.vector.memset(scale_table[:].rearrange("p o t -> p (o t)").bitcast(I32), 0)
 
         nc.sync.dma_start(word_table[:], w_words[0].rearrange("p t b -> p (t b)").bitcast(I32))
         nc.sync.dma_start(offsets[:], offs)
+        nc.sync.dma_start(weights[:], wt[0].rearrange("(p t) one -> p (t one)", t=PACK))
         for q in range(4):
             nc.sync.dma_start(
                 scale_table[32 * q : 32 * q + 4, :, :].bitcast(I32),
@@ -56,14 +58,15 @@ def tile_attend_gsq_w_kernel(tc, xT, w_words, w_scales, y, wt, xm, offs, out):
             )
         for o in range(PASSES):
             nc.sync.dma_start(xt_raw[o][:], xT[0, 512 * o : 512 * (o + 1), :].rearrange("(p j) r -> p j r", j=PACK))
-        nc.sync.dma_start(weights[:], wt[0].rearrange("(p t) one -> p (t one)", t=PACK))
-        nc.sync.dma_start(y_raw[:], y[0].rearrange("(p t) i -> p t i", t=PACK))
+        y_rows = y[0].rearrange("(p t) i -> p t i", t=PACK)
+        for u in range(2):
+            nc.sync.dma_start(y_raw[u][:], y_rows[:, 2 * u : 2 * u + 2, :])
         xm_rows = xm[0].rearrange("(p t) d -> p t d", t=PACK)
-        for c in range(D // XM_CHUNK):
-            nc.sync.dma_start(xm_raw[c][:], xm_rows[:, :, c * XM_CHUNK : (c + 1) * XM_CHUNK])
+        for c, (lo, hi) in enumerate(XM_CHUNKS):
+            nc.sync.dma_start(xm_raw[c][:], xm_rows[:, :, lo:hi])
 
         for w in range(WINDOWS):
-            nc.vector.memset(windows[w][:], 0.0)
+            nc.vector.memset(windows[w][:].bitcast(I32), 0)
 
         pair_words = keep.tile([P, N], U32, name="pair_words", align_bytes=64)
         nc.vector.tensor_copy(pair_words[:], word_table[:].bitcast(U32).indirect(offsets[:]))
@@ -73,7 +76,6 @@ def tile_attend_gsq_w_kernel(tc, xT, w_words, w_scales, y, wt, xm, offs, out):
         halves = pair_words[:].bitcast(U16).rearrange("p (i o) -> p o i", o=PASSES)
         for o in range(PASSES):
             nc.vector.tensor_copy(w_codes[:, o, :].bitcast(U16), halves[:, o, :])
-        nc.vector.tensor_copy(w_scale[:, 1, :], scale_table[:, 1, :].indirect(offsets[:]))
 
         xt_bf = [keep.tile([P, PACK, P, PACK], BF16, name="xt_bf%d" % o, align_bytes=64) for o in range(PASSES)]
         xt_codes = keep.tile([P, PASSES, R], U32, name="xt_codes", align_bytes=64)
@@ -85,6 +87,8 @@ def tile_attend_gsq_w_kernel(tc, xT, w_words, w_scales, y, wt, xm, offs, out):
             mv = VECTOR_M[o]
             nc.scalar.copy(dst[:, mv:, :, :], src[:, mv:, :, :])
             nc.vector.tensor_copy(dst[:, :mv, :, :], src[:, :mv, :, :])
+            if o == 0:
+                nc.vector.tensor_copy(w_scale[:, 1, :], scale_table[:, 1, :].indirect(offsets[:]))
             for h in range(2):
                 nc.vector.quantize_mx(
                     out=xt_codes[:, o, 256 * h : 256 * (h + 1)].bitcast(E4M3),
@@ -108,7 +112,7 @@ def tile_attend_gsq_w_kernel(tc, xT, w_words, w_scales, y, wt, xm, offs, out):
         g_codes = keep.tile([P, N], U32, name="g_codes", align_bytes=64)
         g_scale = keep.tile([P, N], U8, name="g_scale", align_bytes=64)
         for t in range(PACK):
-            nc.vector.tensor_scalar(yw[:, t, :], y_raw[:, t, :], weights[:, t : t + 1], None, MULT)
+            nc.vector.tensor_scalar(yw[:, t, :], y_raw[t // 2][:, t % 2, :], weights[:, t : t + 1], None, MULT)
         for h in range(2):
             cols = slice(h * HALF, (h + 1) * HALF)
             for t in range(PACK):
@@ -129,48 +133,57 @@ def tile_attend_gsq_w_kernel(tc, xT, w_words, w_scales, y, wt, xm, offs, out):
                 in_=g_bf[:, cols, :].rearrange("p i t -> p (i t)"),
             )
 
-        xm_bf = [keep.tile([P, P, PACK], BF16, name="xm_bf%d" % b, align_bytes=64) for b in range(BLOCKS)]
-        xm_codes = [keep.tile([P, P], U32, name="xm_codes%d" % b, align_bytes=64) for b in range(BLOCKS)]
-        xm_scale = [keep.tile([P, P], U8, name="xm_scale%d" % b, align_bytes=64) for b in range(BLOCKS)]
+        xm_bf = keep.tile([P, D, PACK], BF16, name="xm_bf", align_bytes=64)
+        xm_codes = keep.tile([P, D], U32, name="xm_codes", align_bytes=64)
+        xm_scale = keep.tile([P, D], U8, name="xm_scale", align_bytes=64)
 
-        def prepare(b):
-            c, lo = divmod(b * P, XM_CHUNK)
-            nc.scalar.copy(
-                xm_bf[b][:].rearrange("p (c i) t -> p c t i", i=4),
-                xm_raw[c][:, :, lo : lo + P].rearrange("p t (c i) -> p c t i", i=4),
-            )
+        def pieces(b):
+            return [(0, HALF), (HALF, N)] if b == 0 else [(0, N)]
+
+        def prepare(first, last):
+            for b in range(first, last):
+                c = [lo <= b * P < hi for lo, hi in XM_CHUNKS].index(True)
+                lo = b * P - XM_CHUNKS[c][0]
+                nc.scalar.copy(
+                    xm_bf[:, b * P : (b + 1) * P, :].rearrange("p (c i) t -> p c t i", i=4),
+                    xm_raw[c][:, :, lo : lo + P].rearrange("p t (c i) -> p c t i", i=4),
+                )
+            cols = slice(first * P, last * P)
             nc.vector.quantize_mx(
-                out=xm_codes[b][:].bitcast(E4M3),
-                scales=xm_scale[b][:],
-                in_=xm_bf[b][:].rearrange("p d t -> p (d t)"),
+                out=xm_codes[:, cols].bitcast(E4M3),
+                scales=xm_scale[:, cols],
+                in_=xm_bf[:, cols, :].rearrange("p d t -> p (d t)"),
             )
 
         def multiply(b):
             acc = psum_dw.tile([P, N], F32, name="acc")
             nc.tensor.matmul_mx(
                 out=acc[:],
-                lhsT=xm_codes[b][:].bitcast(E4M3),
-                lhsT_scale=xm_scale[b][:],
+                lhsT=xm_codes[:, b * P : (b + 1) * P].bitcast(E4M3),
+                lhsT_scale=xm_scale[:, b * P : (b + 1) * P],
                 rhs=g_codes[:].bitcast(E5M2),
                 rhs_scale=g_scale[:],
                 start=True,
                 stop=True,
             )
             dense = ring.tile([P, N], F32, name="dense", align_bytes=64)
-            nc.scalar.copy(dense[:], acc[:])
+            for lo, hi in pieces(b):
+                nc.scalar.copy(dense[:, lo:hi], acc[:, lo:hi])
             return dense
 
         def place(b, dense):
             window = windows[b % WINDOWS]
-            nc.vector.tensor_copy(window[:].indirect(offsets[:]), dense[:])
+            for lo, hi in pieces(b):
+                nc.vector.tensor_copy(window[:].indirect(offsets[:, lo // 16 : hi // 16]), dense[:, lo:hi])
             nc.sync.dma_start(out[b * P : (b + 1) * P, :], window[:])
 
-        prepare(0)
+        groups = {first: (first, last) for first, last in XM_GROUPS}
+        prepare(*groups[0])
         dense = multiply(0)
-        prepare(1)
+        prepare(*groups[1])
         for b in range(BLOCKS):
             following = multiply(b + 1) if b + 1 < BLOCKS else None
             place(b, dense)
-            if b + 2 < BLOCKS:
-                prepare(b + 2)
+            if b + 2 in groups:
+                prepare(*groups[b + 2])
             dense = following

@@ -22,11 +22,11 @@ P = 128
 PACK = 4
 PASSES = D // (P * PACK)
 BLOCKS = D // P
-XM_CHUNKS = ((0, 256), (256, 512), (512, 1024))
-XM_GROUPS = ((0, 1), (1, 2), (2, 4), (4, 6), (6, 8))
 WINDOWS = 3
-VECTOR_M = (40, 84)
+VECTOR_M = (76, 56)
 HALF = N // 2
+XM_CHUNKS = ((0, 384), (384, 1024))
+QUANT_T = (2, 1)
 
 
 def tile_attend_gsq_w_kernel(tc, xT, w_words, w_scales, y, wt, xm, offs, out):
@@ -40,8 +40,10 @@ def tile_attend_gsq_w_kernel(tc, xT, w_words, w_scales, y, wt, xm, offs, out):
         offsets = keep.tile([P, N // 16], U16, name="offsets")
         word_table = keep.tile([P, T], I32, name="word_table", align_bytes=64)
         scale_table = keep.tile([P, PASSES, T], U8, name="scale_table", align_bytes=64)
-        weights = keep.tile([P, PACK], F32, name="weights")
-        xt_raw = [keep.tile([P, PACK, R], F32, name="xt_raw%d" % o, align_bytes=64) for o in range(PASSES)]
+        weights = keep.tile([P, PACK], F32, name="weights", tag="weights_then_xm", align_bytes=64)
+        xt_raw = [
+            keep.tile([P, PACK, R], F32, name="xt_raw%d" % o, tag="xt_raw%d" % o, align_bytes=64) for o in range(PASSES)
+        ]
         y_raw = [keep.tile([P, 2, N], F32, name="y_raw%d" % u, align_bytes=64) for u in range(2)]
         xm_raw = [keep.tile([P, PACK, hi - lo], F32, name="xm_raw%d" % lo, align_bytes=64) for lo, hi in XM_CHUNKS]
         windows = [keep.tile([P, T], F32, name="window%d" % w, align_bytes=64) for w in range(WINDOWS)]
@@ -70,44 +72,47 @@ def tile_attend_gsq_w_kernel(tc, xT, w_words, w_scales, y, wt, xm, offs, out):
 
         pair_words = keep.tile([P, N], U32, name="pair_words", align_bytes=64)
         nc.vector.tensor_copy(pair_words[:], word_table[:].bitcast(U32).indirect(offsets[:]))
-        w_scale = keep.tile([P, PASSES, N], U8, name="w_scale", align_bytes=64)
-        nc.vector.tensor_copy(w_scale[:, 0, :], scale_table[:, 0, :].indirect(offsets[:]))
+
+        w_scale = [keep.tile([P, N], U8, name="w_scale0", align_bytes=64)]
+        nc.vector.tensor_copy(w_scale[0][:], scale_table[:, 0, :].indirect(offsets[:]))
         w_codes = keep.tile([P, PASSES, 2 * N], U8, name="w_codes", align_bytes=64)
         halves = pair_words[:].bitcast(U16).rearrange("p (i o) -> p o i", o=PASSES)
         for o in range(PASSES):
             nc.vector.tensor_copy(w_codes[:, o, :].bitcast(U16), halves[:, o, :])
 
-        xt_bf = [keep.tile([P, PACK, P, PACK], BF16, name="xt_bf%d" % o, align_bytes=64) for o in range(PASSES)]
         xt_codes = keep.tile([P, PASSES, R], U32, name="xt_codes", align_bytes=64)
         xt_scale = keep.tile([P, PASSES, R], U8, name="xt_scale", align_bytes=64)
         banks = [psum_a.tile([P, N], F32, name="a%d" % t) for t in range(PACK)]
         for o in range(PASSES):
+            xt_bf = keep.tile([P, PACK, P, PACK], BF16, name="xt_bf%d" % o, tag="xt_bf", align_bytes=64)
             src = xt_raw[o][:].rearrange("p j (m t) -> p m j t", t=PACK)
-            dst = xt_bf[o][:].rearrange("p t m j -> p m j t")
+            dst = xt_bf[:].rearrange("p t m j -> p m j t")
             mv = VECTOR_M[o]
             nc.scalar.copy(dst[:, mv:, :, :], src[:, mv:, :, :])
             nc.vector.tensor_copy(dst[:, :mv, :, :], src[:, :mv, :, :])
-            if o == 0:
-                nc.vector.tensor_copy(w_scale[:, 1, :], scale_table[:, 1, :].indirect(offsets[:]))
-            for h in range(2):
+            step = QUANT_T[o]
+            for t in range(0, PACK, step):
                 nc.vector.quantize_mx(
-                    out=xt_codes[:, o, 256 * h : 256 * (h + 1)].bitcast(E4M3),
-                    scales=xt_scale[:, o, 256 * h : 256 * (h + 1)],
-                    in_=xt_bf[o][:, 2 * h : 2 * h + 2, :, :].rearrange("p t m j -> p (t m j)"),
+                    out=xt_codes[:, o, P * t : P * (t + step)].bitcast(E4M3),
+                    scales=xt_scale[:, o, P * t : P * (t + step)],
+                    in_=xt_bf[:, t : t + step, :, :].rearrange("p t m j -> p (t m j)"),
                 )
+            if o == 0:
+                w_scale.append(keep.tile([P, N], U8, name="w_scale1", tag="xt_raw0", align_bytes=64))
+                nc.vector.tensor_copy(w_scale[1][:], scale_table[:, 1, :].indirect(offsets[:]))
             for t in range(PACK):
                 nc.tensor.matmul_mx(
                     out=banks[t][:],
                     lhsT=xt_codes[:, o, P * t : P * (t + 1)].bitcast(E4M3),
                     lhsT_scale=xt_scale[:, o, P * t : P * (t + 1)],
                     rhs=w_codes[:, o, :].bitcast(E2M1),
-                    rhs_scale=w_scale[:, o, :],
+                    rhs_scale=w_scale[o][:],
                     start=(o == 0),
                     stop=(o == PASSES - 1),
                 )
 
         aw = [keep.tile([P, PACK, HALF], F32, name="aw%d" % h, align_bytes=64) for h in range(2)]
-        yw = keep.tile([P, PACK, N], F32, name="yw", align_bytes=64)
+        yw = keep.tile([P, PACK, N], F32, name="yw", tag="xt_bf", align_bytes=64)
         g_bf = keep.tile([P, N, PACK], BF16, name="g_bf", align_bytes=64)
         g_codes = keep.tile([P, N], U32, name="g_codes", align_bytes=64)
         g_scale = keep.tile([P, N], U8, name="g_scale", align_bytes=64)
@@ -132,28 +137,25 @@ def tile_attend_gsq_w_kernel(tc, xT, w_words, w_scales, y, wt, xm, offs, out):
                 scales=g_scale[:, cols],
                 in_=g_bf[:, cols, :].rearrange("p i t -> p (i t)"),
             )
-
-        xm_bf = keep.tile([P, D, PACK], BF16, name="xm_bf", align_bytes=64)
         xm_codes = keep.tile([P, D], U32, name="xm_codes", align_bytes=64)
         xm_scale = keep.tile([P, D], U8, name="xm_scale", align_bytes=64)
 
-        def pieces(b):
-            return [(0, HALF), (HALF, N)] if b == 0 else [(0, N)]
-
-        def prepare(first, last):
+        def prepare(first, last, rounded):
             for b in range(first, last):
                 c = [lo <= b * P < hi for lo, hi in XM_CHUNKS].index(True)
                 lo = b * P - XM_CHUNKS[c][0]
                 nc.scalar.copy(
-                    xm_bf[:, b * P : (b + 1) * P, :].rearrange("p (c i) t -> p c t i", i=4),
+                    rounded[:, (b - first) * P : (b - first + 1) * P, :].rearrange("p (c i) t -> p c t i", i=4),
                     xm_raw[c][:, :, lo : lo + P].rearrange("p t (c i) -> p c t i", i=4),
                 )
             cols = slice(first * P, last * P)
             nc.vector.quantize_mx(
                 out=xm_codes[:, cols].bitcast(E4M3),
                 scales=xm_scale[:, cols],
-                in_=xm_bf[:, cols, :].rearrange("p d t -> p (d t)"),
+                in_=rounded.rearrange("p d t -> p (d t)"),
             )
+
+        dense = {}
 
         def multiply(b):
             acc = psum_dw.tile([P, N], F32, name="acc")
@@ -166,24 +168,32 @@ def tile_attend_gsq_w_kernel(tc, xT, w_words, w_scales, y, wt, xm, offs, out):
                 start=True,
                 stop=True,
             )
-            dense = ring.tile([P, N], F32, name="dense", align_bytes=64)
-            for lo, hi in pieces(b):
-                nc.scalar.copy(dense[:, lo:hi], acc[:, lo:hi])
-            return dense
+            if b == 0:
+                first = keep.tile([P, HALF], F32, name="first_half", tag="dense_then_xm", align_bytes=64)
+                second = ring.tile([P, HALF], F32, name="second_half", tag="dense", align_bytes=64)
+                dense[b] = [(0, HALF, first), (HALF, N, second)]
+            else:
+                whole = ring.tile([P, N], F32, name="whole", tag="dense", align_bytes=64)
+                dense[b] = [(0, N, whole)]
+            for lo, hi, piece in dense[b]:
+                nc.scalar.copy(piece[:], acc[:, lo:hi])
 
-        def place(b, dense):
+        def place(b):
             window = windows[b % WINDOWS]
-            for lo, hi in pieces(b):
-                nc.vector.tensor_copy(window[:].indirect(offsets[:, lo // 16 : hi // 16]), dense[:, lo:hi])
+            for lo, hi, piece in dense[b]:
+                nc.vector.tensor_copy(window[:].indirect(offsets[:, lo // 16 : hi // 16]), piece[:])
             nc.sync.dma_start(out[b * P : (b + 1) * P, :], window[:])
 
-        groups = {first: (first, last) for first, last in XM_GROUPS}
-        prepare(*groups[0])
-        dense = multiply(0)
-        prepare(*groups[1])
-        for b in range(BLOCKS):
-            following = multiply(b + 1) if b + 1 < BLOCKS else None
-            place(b, dense)
-            if b + 2 in groups:
-                prepare(*groups[b + 2])
-            dense = following
+        xm_early = keep.tile([P, 3 * P, PACK], BF16, name="xm_early", tag="weights_then_xm", align_bytes=64)
+        for b in range(3):
+            prepare(b, b + 1, xm_early[:, b * P : (b + 1) * P, :])
+            if b < 2:
+                multiply(b)
+        place(0)
+        xm_late = keep.tile([P, 5 * P, PACK], BF16, name="xm_late", tag="dense_then_xm", align_bytes=64)
+        for first, last in ((3, 5), (5, 7), (7, 8)):
+            prepare(first, last, xm_late[:, (first - 3) * P : (last - 3) * P, :])
+        for b in range(1, BLOCKS):
+            if b + 1 < BLOCKS:
+                multiply(b + 1)
+            place(b)

@@ -25,7 +25,7 @@ BLOCKS = D // P
 WINDOWS = 3
 VECTOR_M = (76, 56)
 HALF = N // 2
-XM_CHUNKS = ((0, 384), (384, 1024))
+XM_CHUNKS = ((0, 128), (128, 512), (512, 1024))
 QUANT_T = (2, 1)
 
 
@@ -67,6 +67,10 @@ def tile_attend_gsq_w_kernel(tc, xT, w_words, w_scales, y, wt, xm, offs, out):
         for c, (lo, hi) in enumerate(XM_CHUNKS):
             nc.sync.dma_start(xm_raw[c][:], xm_rows[:, :, lo:hi])
 
+        g_codes = keep.tile([P, HALF + N], U32, name="g_codes", align_bytes=64)
+        g_scale = keep.tile([P, HALF + N], U8, name="g_scale", align_bytes=64)
+        nc.vector.memset(g_codes[:, :HALF].bitcast(I32), 0)
+        nc.vector.memset(g_scale[:, :HALF].bitcast(I32), 0)
         for w in range(WINDOWS):
             nc.vector.memset(windows[w][:].bitcast(I32), 0)
 
@@ -80,7 +84,7 @@ def tile_attend_gsq_w_kernel(tc, xT, w_words, w_scales, y, wt, xm, offs, out):
         for o in range(PASSES):
             nc.vector.tensor_copy(w_codes[:, o, :].bitcast(U16), halves[:, o, :])
 
-        xt_codes = keep.tile([P, PASSES, R], U32, name="xt_codes", align_bytes=64)
+        xt_codes = keep.tile([P, PASSES, R], U32, name="xt_codes", tag="xt_codes_then_xm", align_bytes=64)
         xt_scale = keep.tile([P, PASSES, R], U8, name="xt_scale", align_bytes=64)
         banks = [psum_a.tile([P, N], F32, name="a%d" % t) for t in range(PACK)]
         for o in range(PASSES):
@@ -111,18 +115,21 @@ def tile_attend_gsq_w_kernel(tc, xT, w_words, w_scales, y, wt, xm, offs, out):
                     stop=(o == PASSES - 1),
                 )
 
-        aw = [keep.tile([P, PACK, HALF], F32, name="aw%d" % h, align_bytes=64) for h in range(2)]
+        aw = [
+            keep.tile([P, PACK, HALF], F32, name="aw%d" % h, tag="aw%d_then_xm" % h, align_bytes=64) for h in range(2)
+        ]
         yw = keep.tile([P, PACK, N], F32, name="yw", tag="xt_bf", align_bytes=64)
         g_bf = keep.tile([P, N, PACK], BF16, name="g_bf", align_bytes=64)
-        g_codes = keep.tile([P, N], U32, name="g_codes", align_bytes=64)
-        g_scale = keep.tile([P, N], U8, name="g_scale", align_bytes=64)
-        for t in range(PACK):
-            nc.vector.tensor_scalar(yw[:, t, :], y_raw[t // 2][:, t % 2, :], weights[:, t : t + 1], None, MULT)
-        for h in range(2):
-            cols = slice(h * HALF, (h + 1) * HALF)
+        xm_codes = keep.tile([P, D], U32, name="xm_codes", align_bytes=64)
+        xm_scale = keep.tile([P, D], U8, name="xm_scale", align_bytes=64)
+
+        def weigh_a(h):
             for t in range(PACK):
-                nc.scalar.activation(aw[h][:, t, :], banks[t][:, cols], COPY, scale=weights[:, t : t + 1])
-        for h in range(2):
+                nc.scalar.activation(
+                    aw[h][:, t, :], banks[t][:, h * HALF : (h + 1) * HALF], COPY, scale=weights[:, t : t + 1]
+                )
+
+        def subtract(h):
             cols = slice(h * HALF, (h + 1) * HALF)
             nc.vector.tensor_tensor(
                 g_bf[:, cols, :].rearrange("p (c i) t -> p c t i", i=4),
@@ -130,17 +137,17 @@ def tile_attend_gsq_w_kernel(tc, xT, w_words, w_scales, y, wt, xm, offs, out):
                 yw[:, :, cols].rearrange("p t (c i) -> p c t i", i=4),
                 SUB,
             )
-        for h in range(2):
-            cols = slice(h * HALF, (h + 1) * HALF)
+
+        def quantise_g(h):
+            cols = slice((h + 1) * HALF, (h + 2) * HALF)
             nc.vector.quantize_mx(
                 out=g_codes[:, cols].bitcast(E5M2),
                 scales=g_scale[:, cols],
-                in_=g_bf[:, cols, :].rearrange("p i t -> p (i t)"),
+                in_=g_bf[:, h * HALF : (h + 1) * HALF, :].rearrange("p i t -> p (i t)"),
             )
-        xm_codes = keep.tile([P, D], U32, name="xm_codes", align_bytes=64)
-        xm_scale = keep.tile([P, D], U8, name="xm_scale", align_bytes=64)
 
-        def prepare(first, last, rounded):
+        def round_xm(first, last, tag):
+            rounded = keep.tile([P, (last - first) * P, PACK], BF16, name="xm_bf%d" % first, tag=tag, align_bytes=64)
             for b in range(first, last):
                 c = [lo <= b * P < hi for lo, hi in XM_CHUNKS].index(True)
                 lo = b * P - XM_CHUNKS[c][0]
@@ -148,6 +155,9 @@ def tile_attend_gsq_w_kernel(tc, xT, w_words, w_scales, y, wt, xm, offs, out):
                     rounded[:, (b - first) * P : (b - first + 1) * P, :].rearrange("p (c i) t -> p c t i", i=4),
                     xm_raw[c][:, :, lo : lo + P].rearrange("p t (c i) -> p c t i", i=4),
                 )
+            return rounded
+
+        def quantise_xm(first, last, rounded):
             cols = slice(first * P, last * P)
             nc.vector.quantize_mx(
                 out=xm_codes[:, cols].bitcast(E4M3),
@@ -155,45 +165,61 @@ def tile_attend_gsq_w_kernel(tc, xT, w_words, w_scales, y, wt, xm, offs, out):
                 in_=rounded.rearrange("p d t -> p (d t)"),
             )
 
-        dense = {}
-
-        def multiply(b):
+        def multiply(b, start, lo, hi, piece):
             acc = psum_dw.tile([P, N], F32, name="acc")
             nc.tensor.matmul_mx(
                 out=acc[:],
                 lhsT=xm_codes[:, b * P : (b + 1) * P].bitcast(E4M3),
                 lhsT_scale=xm_scale[:, b * P : (b + 1) * P],
-                rhs=g_codes[:].bitcast(E5M2),
-                rhs_scale=g_scale[:],
+                rhs=g_codes[:, start : start + N].bitcast(E5M2),
+                rhs_scale=g_scale[:, start : start + N],
                 start=True,
                 stop=True,
             )
-            if b == 0:
-                first = keep.tile([P, HALF], F32, name="first_half", tag="dense_then_xm", align_bytes=64)
-                second = ring.tile([P, HALF], F32, name="second_half", tag="dense", align_bytes=64)
-                dense[b] = [(0, HALF, first), (HALF, N, second)]
-            else:
-                whole = ring.tile([P, N], F32, name="whole", tag="dense", align_bytes=64)
-                dense[b] = [(0, N, whole)]
-            for lo, hi, piece in dense[b]:
-                nc.scalar.copy(piece[:], acc[:, lo:hi])
+            nc.scalar.copy(piece[:], acc[:, lo:hi])
 
-        def place(b):
-            window = windows[b % WINDOWS]
-            for lo, hi, piece in dense[b]:
-                nc.vector.tensor_copy(window[:].indirect(offsets[:, lo // 16 : hi // 16]), piece[:])
-            nc.sync.dma_start(out[b * P : (b + 1) * P, :], window[:])
+        def scatter(b, lo, hi, piece):
+            nc.vector.tensor_copy(windows[b % WINDOWS][:].indirect(offsets[:, lo // 16 : hi // 16]), piece[:])
 
-        xm_early = keep.tile([P, 3 * P, PACK], BF16, name="xm_early", tag="weights_then_xm", align_bytes=64)
-        for b in range(3):
-            prepare(b, b + 1, xm_early[:, b * P : (b + 1) * P, :])
-            if b < 2:
-                multiply(b)
-        place(0)
-        xm_late = keep.tile([P, 5 * P, PACK], BF16, name="xm_late", tag="dense_then_xm", align_bytes=64)
-        for first, last in ((3, 5), (5, 7), (7, 8)):
-            prepare(first, last, xm_late[:, (first - 3) * P : (last - 3) * P, :])
-        for b in range(1, BLOCKS):
+        def store(b):
+            nc.sync.dma_start(out[b * P : (b + 1) * P, :], windows[b % WINDOWS][:])
+
+        dense = {}
+
+        def multiply_whole(b):
+            dense[b] = ring.tile([P, N], F32, name="whole", tag="dense", align_bytes=64)
+            multiply(b, HALF, 0, N, dense[b])
+
+        for t in range(PACK):
+            nc.vector.tensor_scalar(yw[:, t, :], y_raw[t // 2][:, t % 2, :], weights[:, t : t + 1], None, MULT)
+        weigh_a(0)
+        rounded0 = round_xm(0, 1, "xt_codes_then_xm")
+        weigh_a(1)
+        rounded1 = round_xm(1, 2, "weights_then_xm")
+        subtract(0)
+        quantise_xm(0, 1, rounded0[:])
+        quantise_g(0)
+        first_half = keep.tile([P, HALF], F32, name="first_half", tag="dense_then_xm", align_bytes=64)
+        multiply(0, 0, HALF, N, first_half)
+        subtract(1)
+        quantise_xm(1, 2, rounded1[:])
+        quantise_g(1)
+        second_half = ring.tile([P, HALF], F32, name="second_half", tag="dense", align_bytes=64)
+        multiply(0, HALF, HALF, N, second_half)
+        multiply_whole(1)
+        rounded23 = round_xm(2, 4, "aw1_then_xm")
+        scatter(0, 0, HALF, first_half)
+        quantise_xm(2, 4, rounded23[:])
+        scatter(0, HALF, N, second_half)
+        store(0)
+        late = round_xm(4, 8, "dense_then_xm")
+        multiply_whole(2)
+        scatter(1, 0, N, dense[1])
+        store(1)
+        quantise_xm(4, 6, late[:, : 2 * P, :])
+        quantise_xm(6, 8, late[:, 2 * P :, :])
+        for b in range(2, BLOCKS):
             if b + 1 < BLOCKS:
-                multiply(b + 1)
-            place(b)
+                multiply_whole(b + 1)
+            scatter(b, 0, N, dense[b])
+            store(b)

@@ -23,7 +23,7 @@ PACK = 4
 PASSES = D // (P * PACK)
 BLOCKS = D // P
 WINDOWS = 3
-VECTOR_M = (76, 56)
+VECTOR_M = (76, 76)
 HALF = N // 2
 XM_CHUNKS = ((0, 128), (128, 512), (512, 1024))
 QUANT_T = (2, 1)
@@ -39,32 +39,36 @@ def tile_attend_gsq_w_kernel(tc, xT, w_words, w_scales, y, wt, xm, offs, out):
 
         offsets = keep.tile([P, N // 16], U16, name="offsets")
         word_table = keep.tile([P, T], I32, name="word_table", align_bytes=64)
-        scale_table = keep.tile([P, PASSES, T], U8, name="scale_table", align_bytes=64)
+        scale_table = keep.tile([P, T], U8, name="scale_table", tag="scales_then_y", align_bytes=64)
         weights = keep.tile([P, PACK], F32, name="weights", tag="weights_then_xm", align_bytes=64)
         xt_raw = [
             keep.tile([P, PACK, R], F32, name="xt_raw%d" % o, tag="xt_raw%d" % o, align_bytes=64) for o in range(PASSES)
         ]
-        y_raw = [keep.tile([P, 2, N], F32, name="y_raw%d" % u, align_bytes=64) for u in range(2)]
-        xm_raw = [keep.tile([P, PACK, hi - lo], F32, name="xm_raw%d" % lo, align_bytes=64) for lo, hi in XM_CHUNKS]
         windows = [keep.tile([P, T], F32, name="window%d" % w, align_bytes=64) for w in range(WINDOWS)]
 
-        nc.vector.memset(scale_table[:].rearrange("p o t -> p (o t)").bitcast(I32), 0)
+        second_plane = keep.tile([P, N], U8, name="second_plane", align_bytes=64)
+        nc.vector.memset(scale_table[:].bitcast(I32), 0)
+        nc.vector.memset(second_plane[:].bitcast(I32), 0)
 
-        nc.sync.dma_start(word_table[:], w_words[0].rearrange("p t b -> p (t b)").bitcast(I32))
         nc.sync.dma_start(offsets[:], offs)
-        nc.sync.dma_start(weights[:], wt[0].rearrange("(p t) one -> p (t one)", t=PACK))
+        nc.scalar.dma_start(weights[:], wt[0].rearrange("(p t) one -> p (t one)", t=PACK))
+        nc.sync.dma_start(word_table[:], w_words[0].rearrange("p t b -> p (t b)").bitcast(I32))
         for q in range(4):
             nc.sync.dma_start(
-                scale_table[32 * q : 32 * q + 4, :, :].bitcast(I32),
-                w_scales[:, 4 * q : 4 * q + 4, :].rearrange("o f t -> f o t").bitcast(I32),
+                scale_table[32 * q : 32 * q + 4, :].bitcast(I32), w_scales[0, 4 * q : 4 * q + 4, :].bitcast(I32)
             )
+        nc.sync.dma_start(scale_table[4:20, :].bitcast(I32), w_scales[1].bitcast(I32))
         for o in range(PASSES):
             nc.sync.dma_start(xt_raw[o][:], xT[0, 512 * o : 512 * (o + 1), :].rearrange("(p j) r -> p j r", j=PACK))
         y_rows = y[0].rearrange("(p t) i -> p t i", t=PACK)
-        for u in range(2):
-            nc.sync.dma_start(y_raw[u][:], y_rows[:, 2 * u : 2 * u + 2, :])
         xm_rows = xm[0].rearrange("(p t) d -> p t d", t=PACK)
-        for c, (lo, hi) in enumerate(XM_CHUNKS):
+        y_raw = [keep.tile([P, 2, N], F32, name="y_raw0", align_bytes=64)]
+        nc.sync.dma_start(y_raw[0][:], y_rows[:, 0:2, :])
+        xm_raw = []
+
+        def load_xm(c, tag):
+            lo, hi = XM_CHUNKS[c]
+            xm_raw.append(keep.tile([P, PACK, hi - lo], F32, name="xm_raw%d" % c, tag=tag, align_bytes=64))
             nc.sync.dma_start(xm_raw[c][:], xm_rows[:, :, lo:hi])
 
         g_codes = keep.tile([P, HALF + N], U32, name="g_codes", align_bytes=64)
@@ -74,15 +78,21 @@ def tile_attend_gsq_w_kernel(tc, xT, w_words, w_scales, y, wt, xm, offs, out):
         for w in range(WINDOWS):
             nc.vector.memset(windows[w][:].bitcast(I32), 0)
 
-        pair_words = keep.tile([P, N], U32, name="pair_words", align_bytes=64)
+        pair_words = keep.tile([P, N], U32, name="pair_words", tag="pairs_then_xm", align_bytes=64)
         nc.vector.tensor_copy(pair_words[:], word_table[:].bitcast(U32).indirect(offsets[:]))
 
-        w_scale = [keep.tile([P, N], U8, name="w_scale0", align_bytes=64)]
-        nc.vector.tensor_copy(w_scale[0][:], scale_table[:, 0, :].indirect(offsets[:]))
+        both_planes = keep.tile([P, N], U8, name="both_planes", align_bytes=64)
+        nc.vector.tensor_copy(both_planes[:], scale_table[:].indirect(offsets[:]))
+        for q in range(4):
+            nc.scalar.dma_start(
+                second_plane[32 * q : 32 * q + 4, :].bitcast(I32), both_planes[4 + 4 * q : 8 + 4 * q, :].bitcast(I32)
+            )
+        w_scale = [both_planes, second_plane]
+        y_raw.append(keep.tile([P, 2, N], F32, name="y_raw1", tag="scales_then_y", align_bytes=64))
+        nc.sync.dma_start(y_raw[1][:], y_rows[:, 2:4, :])
         w_codes = keep.tile([P, PASSES, 2 * N], U8, name="w_codes", align_bytes=64)
         halves = pair_words[:].bitcast(U16).rearrange("p (i o) -> p o i", o=PASSES)
-        for o in range(PASSES):
-            nc.vector.tensor_copy(w_codes[:, o, :].bitcast(U16), halves[:, o, :])
+        nc.vector.tensor_copy(w_codes[:, 0, :].bitcast(U16), halves[:, 0, :])
 
         xt_codes = keep.tile([P, PASSES, R], U32, name="xt_codes", tag="xt_codes_then_xm", align_bytes=64)
         xt_scale = keep.tile([P, PASSES, R], U8, name="xt_scale", align_bytes=64)
@@ -94,6 +104,12 @@ def tile_attend_gsq_w_kernel(tc, xT, w_words, w_scales, y, wt, xm, offs, out):
             mv = VECTOR_M[o]
             nc.scalar.copy(dst[:, mv:, :, :], src[:, mv:, :, :])
             nc.vector.tensor_copy(dst[:, :mv, :, :], src[:, :mv, :, :])
+            if o == 0:
+                nc.vector.tensor_copy(w_codes[:, 1, :].bitcast(U16), halves[:, 1, :])
+                load_xm(0, "xt_raw0")
+                load_xm(1, "pairs_then_xm")
+            else:
+                load_xm(2, "xt_raw1")
             step = QUANT_T[o]
             for t in range(0, PACK, step):
                 nc.vector.quantize_mx(
@@ -101,9 +117,6 @@ def tile_attend_gsq_w_kernel(tc, xT, w_words, w_scales, y, wt, xm, offs, out):
                     scales=xt_scale[:, o, P * t : P * (t + step)],
                     in_=xt_bf[:, t : t + step, :, :].rearrange("p t m j -> p (t m j)"),
                 )
-            if o == 0:
-                w_scale.append(keep.tile([P, N], U8, name="w_scale1", tag="xt_raw0", align_bytes=64))
-                nc.vector.tensor_copy(w_scale[1][:], scale_table[:, 1, :].indirect(offsets[:]))
             for t in range(PACK):
                 nc.tensor.matmul_mx(
                     out=banks[t][:],

@@ -23,7 +23,7 @@ PACK = 4
 PASSES = D // (P * PACK)
 BLOCKS = D // P
 WINDOWS = 3
-VECTOR_M = (76, 76)
+VECTOR_M = (84, 48)
 HALF = N // 2
 XM_CHUNKS = ((0, 128), (128, 512), (512, 1024))
 QUANT_T = (2, 1)
@@ -39,36 +39,35 @@ def tile_attend_gsq_w_kernel(tc, xT, w_words, w_scales, y, wt, xm, offs, out):
 
         offsets = keep.tile([P, N // 16], U16, name="offsets")
         word_table = keep.tile([P, T], I32, name="word_table", align_bytes=64)
-        scale_table = keep.tile([P, T], U8, name="scale_table", tag="scales_then_y", align_bytes=64)
+        scale_table = [keep.tile([P, T], U8, name="scale_table%d" % o, align_bytes=64) for o in range(PASSES)]
         weights = keep.tile([P, PACK], F32, name="weights", tag="weights_then_xm", align_bytes=64)
         xt_raw = [
             keep.tile([P, PACK, R], F32, name="xt_raw%d" % o, tag="xt_raw%d" % o, align_bytes=64) for o in range(PASSES)
         ]
+        y_raw = [keep.tile([P, 2, N], F32, name="y_raw%d" % u, align_bytes=64) for u in range(2)]
+        xm_raw = [
+            keep.tile([P, PACK, hi - lo], F32, name="xm_raw%d" % lo, tag="xm_raw%d" % lo, align_bytes=64)
+            for lo, hi in XM_CHUNKS
+        ]
         windows = [keep.tile([P, T], F32, name="window%d" % w, align_bytes=64) for w in range(WINDOWS)]
 
-        second_plane = keep.tile([P, N], U8, name="second_plane", align_bytes=64)
-        nc.vector.memset(scale_table[:].bitcast(I32), 0)
-        nc.vector.memset(second_plane[:].bitcast(I32), 0)
-
-        nc.sync.dma_start(offsets[:], offs)
-        nc.scalar.dma_start(weights[:], wt[0].rearrange("(p t) one -> p (t one)", t=PACK))
-        nc.sync.dma_start(word_table[:], w_words[0].rearrange("p t b -> p (t b)").bitcast(I32))
-        for q in range(4):
-            nc.sync.dma_start(
-                scale_table[32 * q : 32 * q + 4, :].bitcast(I32), w_scales[0, 4 * q : 4 * q + 4, :].bitcast(I32)
-            )
-        nc.sync.dma_start(scale_table[4:20, :].bitcast(I32), w_scales[1].bitcast(I32))
         for o in range(PASSES):
-            nc.sync.dma_start(xt_raw[o][:], xT[0, 512 * o : 512 * (o + 1), :].rearrange("(p j) r -> p j r", j=PACK))
-        y_rows = y[0].rearrange("(p t) i -> p t i", t=PACK)
-        xm_rows = xm[0].rearrange("(p t) d -> p t d", t=PACK)
-        y_raw = [keep.tile([P, 2, N], F32, name="y_raw0", align_bytes=64)]
-        nc.sync.dma_start(y_raw[0][:], y_rows[:, 0:2, :])
-        xm_raw = []
+            nc.vector.memset(scale_table[o][:].bitcast(I32), 0)
 
-        def load_xm(c, tag):
-            lo, hi = XM_CHUNKS[c]
-            xm_raw.append(keep.tile([P, PACK, hi - lo], F32, name="xm_raw%d" % c, tag=tag, align_bytes=64))
+        nc.sync.dma_start(word_table[:], w_words[0].rearrange("p t b -> p (t b)").bitcast(I32))
+        nc.sync.dma_start(offsets[:], offs)
+        for o in range(PASSES):
+            for q in range(4):
+                nc.sync.dma_start(
+                    scale_table[o][32 * q : 32 * q + 4, :].bitcast(I32), w_scales[o, 4 * q : 4 * q + 4, :].bitcast(I32)
+                )
+            nc.sync.dma_start(xt_raw[o][:], xT[0, 512 * o : 512 * (o + 1), :].rearrange("(p j) r -> p j r", j=PACK))
+        nc.sync.dma_start(weights[:], wt[0].rearrange("(p t) one -> p (t one)", t=PACK))
+        y_rows = y[0].rearrange("(p t) i -> p t i", t=PACK)
+        for u in range(2):
+            nc.sync.dma_start(y_raw[u][:], y_rows[:, 2 * u : 2 * u + 2, :])
+        xm_rows = xm[0].rearrange("(p t) d -> p t d", t=PACK)
+        for c, (lo, hi) in enumerate(XM_CHUNKS):
             nc.sync.dma_start(xm_raw[c][:], xm_rows[:, :, lo:hi])
 
         g_codes = keep.tile([P, HALF + N], U32, name="g_codes", align_bytes=64)
@@ -78,18 +77,11 @@ def tile_attend_gsq_w_kernel(tc, xT, w_words, w_scales, y, wt, xm, offs, out):
         for w in range(WINDOWS):
             nc.vector.memset(windows[w][:].bitcast(I32), 0)
 
-        pair_words = keep.tile([P, N], U32, name="pair_words", tag="pairs_then_xm", align_bytes=64)
+        pair_words = keep.tile([P, N], U32, name="pair_words", align_bytes=64)
         nc.vector.tensor_copy(pair_words[:], word_table[:].bitcast(U32).indirect(offsets[:]))
 
-        both_planes = keep.tile([P, N], U8, name="both_planes", align_bytes=64)
-        nc.vector.tensor_copy(both_planes[:], scale_table[:].indirect(offsets[:]))
-        for q in range(4):
-            nc.scalar.dma_start(
-                second_plane[32 * q : 32 * q + 4, :].bitcast(I32), both_planes[4 + 4 * q : 8 + 4 * q, :].bitcast(I32)
-            )
-        w_scale = [both_planes, second_plane]
-        y_raw.append(keep.tile([P, 2, N], F32, name="y_raw1", tag="scales_then_y", align_bytes=64))
-        nc.sync.dma_start(y_raw[1][:], y_rows[:, 2:4, :])
+        w_scale = [keep.tile([P, N], U8, name="w_scale0", align_bytes=64)]
+        nc.vector.tensor_copy(w_scale[0][:], scale_table[0][:].indirect(offsets[:]))
         w_codes = keep.tile([P, PASSES, 2 * N], U8, name="w_codes", align_bytes=64)
         halves = pair_words[:].bitcast(U16).rearrange("p (i o) -> p o i", o=PASSES)
         nc.vector.tensor_copy(w_codes[:, 0, :].bitcast(U16), halves[:, 0, :])
@@ -106,10 +98,6 @@ def tile_attend_gsq_w_kernel(tc, xT, w_words, w_scales, y, wt, xm, offs, out):
             nc.vector.tensor_copy(dst[:, :mv, :, :], src[:, :mv, :, :])
             if o == 0:
                 nc.vector.tensor_copy(w_codes[:, 1, :].bitcast(U16), halves[:, 1, :])
-                load_xm(0, "xt_raw0")
-                load_xm(1, "pairs_then_xm")
-            else:
-                load_xm(2, "xt_raw1")
             step = QUANT_T[o]
             for t in range(0, PACK, step):
                 nc.vector.quantize_mx(
@@ -117,6 +105,9 @@ def tile_attend_gsq_w_kernel(tc, xT, w_words, w_scales, y, wt, xm, offs, out):
                     scales=xt_scale[:, o, P * t : P * (t + step)],
                     in_=xt_bf[:, t : t + step, :, :].rearrange("p t m j -> p (t m j)"),
                 )
+            if o == 0:
+                w_scale.append(keep.tile([P, N], U8, name="w_scale1", tag="xt_raw0", align_bytes=64))
+                nc.vector.tensor_copy(w_scale[1][:], scale_table[1][:].indirect(offsets[:]))
             for t in range(PACK):
                 nc.tensor.matmul_mx(
                     out=banks[t][:],
@@ -128,15 +119,14 @@ def tile_attend_gsq_w_kernel(tc, xT, w_words, w_scales, y, wt, xm, offs, out):
                     stop=(o == PASSES - 1),
                 )
 
-        aw = [
-            keep.tile([P, PACK, HALF], F32, name="aw%d" % h, tag="aw%d_then_xm" % h, align_bytes=64) for h in range(2)
-        ]
+        aw = []
         yw = keep.tile([P, PACK, N], F32, name="yw", tag="xt_bf", align_bytes=64)
         g_bf = keep.tile([P, N, PACK], BF16, name="g_bf", align_bytes=64)
         xm_codes = keep.tile([P, D], U32, name="xm_codes", align_bytes=64)
         xm_scale = keep.tile([P, D], U8, name="xm_scale", align_bytes=64)
 
-        def weigh_a(h):
+        def weigh_a(h, tag):
+            aw.append(keep.tile([P, PACK, HALF], F32, name="aw%d" % h, tag=tag, align_bytes=64))
             for t in range(PACK):
                 nc.scalar.activation(
                     aw[h][:, t, :], banks[t][:, h * HALF : (h + 1) * HALF], COPY, scale=weights[:, t : t + 1]
@@ -203,31 +193,36 @@ def tile_attend_gsq_w_kernel(tc, xT, w_words, w_scales, y, wt, xm, offs, out):
             dense[b] = ring.tile([P, N], F32, name="whole", tag="dense", align_bytes=64)
             multiply(b, HALF, 0, N, dense[b])
 
+        def multiply_half(b, h, tag):
+            piece = keep.tile([P, HALF], F32, name="half%d%d" % (b, h), tag=tag, align_bytes=64)
+            multiply(b, h * HALF, HALF, N, piece)
+            return piece
+
         for t in range(PACK):
             nc.vector.tensor_scalar(yw[:, t, :], y_raw[t // 2][:, t % 2, :], weights[:, t : t + 1], None, MULT)
-        weigh_a(0)
+        weigh_a(0, "aw0")
         rounded0 = round_xm(0, 1, "xt_codes_then_xm")
-        weigh_a(1)
+        weigh_a(1, "xm_raw0")
         rounded1 = round_xm(1, 2, "weights_then_xm")
         subtract(0)
         quantise_xm(0, 1, rounded0[:])
         quantise_g(0)
-        first_half = keep.tile([P, HALF], F32, name="first_half", tag="dense_then_xm", align_bytes=64)
-        multiply(0, 0, HALF, N, first_half)
+        half00 = multiply_half(0, 0, "dense_then_xm")
         subtract(1)
         quantise_xm(1, 2, rounded1[:])
         quantise_g(1)
-        second_half = ring.tile([P, HALF], F32, name="second_half", tag="dense", align_bytes=64)
-        multiply(0, HALF, HALF, N, second_half)
-        multiply_whole(1)
-        rounded23 = round_xm(2, 4, "aw1_then_xm")
-        scatter(0, 0, HALF, first_half)
+        half10 = multiply_half(1, 0, "half10")
+        half01 = multiply_half(0, 1, "half01")
+        half11 = multiply_half(1, 1, "half11")
+        rounded23 = round_xm(2, 4, "xm_raw0")
+        scatter(0, 0, HALF, half00)
         quantise_xm(2, 4, rounded23[:])
-        scatter(0, HALF, N, second_half)
+        scatter(1, 0, HALF, half10)
+        scatter(0, HALF, N, half01)
         store(0)
         late = round_xm(4, 8, "dense_then_xm")
         multiply_whole(2)
-        scatter(1, 0, N, dense[1])
+        scatter(1, HALF, N, half11)
         store(1)
         quantise_xm(4, 6, late[:, : 2 * P, :])
         quantise_xm(6, 8, late[:, 2 * P :, :])

@@ -57,10 +57,8 @@ def tile_attend_gsq_w_kernel(tc, xT, w_words, w_scales, y, wt, xm, offs, out):
         nc.sync.dma_start(word_table[:], w_words[0].rearrange("p t b -> p (t b)").bitcast(I32))
         nc.sync.dma_start(offsets[:], offs)
         for o in range(PASSES):
-            for q in range(4):
-                nc.sync.dma_start(
-                    scale_table[o][32 * q : 32 * q + 4, :].bitcast(I32), w_scales[o, 4 * q : 4 * q + 4, :].bitcast(I32)
-                )
+            for s in range(4):
+                nc.sync.dma_start(scale_table[o][s:P:32, :].bitcast(I32), w_scales[o, s:16:4, :].bitcast(I32))
             nc.sync.dma_start(xt_raw[o][:], xT[0, 512 * o : 512 * (o + 1), :].rearrange("(p j) r -> p j r", j=PACK))
         nc.sync.dma_start(weights[:], wt[0].rearrange("(p t) one -> p (t one)", t=PACK))
         y_rows = y[0].rearrange("(p t) i -> p t i", t=PACK)

@@ -23,9 +23,9 @@ PACK = 4
 PASSES = D // (P * PACK)
 BLOCKS = D // P
 WINDOWS = 3
-VECTOR_M = (84, 48)
+VECTOR_M = (76, 56)
 HALF = N // 2
-XM_CHUNKS = ((0, 128), (128, 512), (512, 1024))
+XM_CHUNKS = ((0, 256), (256, 512), (512, 1024))
 QUANT_T = (2, 1)
 
 
@@ -40,11 +40,11 @@ def tile_attend_gsq_w_kernel(tc, xT, w_words, w_scales, y, wt, xm, offs, out):
         offsets = keep.tile([P, N // 16], U16, name="offsets")
         word_table = keep.tile([P, T], I32, name="word_table", align_bytes=64)
         scale_table = [keep.tile([P, T], U8, name="scale_table%d" % o, align_bytes=64) for o in range(PASSES)]
-        weights = keep.tile([P, PACK], F32, name="weights", tag="weights_then_xm", align_bytes=64)
+        weights = keep.tile([P, PACK], F32, name="weights", align_bytes=64)
         xt_raw = [
             keep.tile([P, PACK, R], F32, name="xt_raw%d" % o, tag="xt_raw%d" % o, align_bytes=64) for o in range(PASSES)
         ]
-        y_raw = [keep.tile([P, 2, N], F32, name="y_raw%d" % u, align_bytes=64) for u in range(2)]
+        y_raw = [keep.tile([P, PACK, HALF], F32, name="y_raw%d" % h, align_bytes=64) for h in range(2)]
         xm_raw = [
             keep.tile([P, PACK, hi - lo], F32, name="xm_raw%d" % lo, tag="xm_raw%d" % lo, align_bytes=64)
             for lo, hi in XM_CHUNKS
@@ -62,10 +62,10 @@ def tile_attend_gsq_w_kernel(tc, xT, w_words, w_scales, y, wt, xm, offs, out):
             nc.sync.dma_start(xt_raw[o][:], xT[0, 512 * o : 512 * (o + 1), :].rearrange("(p j) r -> p j r", j=PACK))
         nc.sync.dma_start(weights[:], wt[0].rearrange("(p t) one -> p (t one)", t=PACK))
         y_rows = y[0].rearrange("(p t) i -> p t i", t=PACK)
-        for u in range(2):
-            nc.sync.dma_start(y_raw[u][:], y_rows[:, 2 * u : 2 * u + 2, :])
         xm_rows = xm[0].rearrange("(p t) d -> p t d", t=PACK)
         for c, (lo, hi) in enumerate(XM_CHUNKS):
+            if c < 2:
+                nc.sync.dma_start(y_raw[c][:], y_rows[:, :, c * HALF : (c + 1) * HALF])
             nc.sync.dma_start(xm_raw[c][:], xm_rows[:, :, lo:hi])
 
         g_codes = keep.tile([P, HALF + N], U32, name="g_codes", align_bytes=64)
@@ -84,7 +84,7 @@ def tile_attend_gsq_w_kernel(tc, xT, w_words, w_scales, y, wt, xm, offs, out):
         halves = pair_words[:].bitcast(U16).rearrange("p (i o) -> p o i", o=PASSES)
         nc.vector.tensor_copy(w_codes[:, 0, :].bitcast(U16), halves[:, 0, :])
 
-        xt_codes = keep.tile([P, PASSES, R], U32, name="xt_codes", tag="xt_codes_then_xm", align_bytes=64)
+        xt_codes = keep.tile([P, PASSES, R], U32, name="xt_codes", align_bytes=64)
         xt_scale = keep.tile([P, PASSES, R], U8, name="xt_scale", align_bytes=64)
         banks = [psum_a.tile([P, N], F32, name="a%d" % t) for t in range(PACK)]
         for o in range(PASSES):
@@ -117,26 +117,33 @@ def tile_attend_gsq_w_kernel(tc, xT, w_words, w_scales, y, wt, xm, offs, out):
                     stop=(o == PASSES - 1),
                 )
 
-        aw = []
-        yw = keep.tile([P, PACK, N], F32, name="yw", tag="xt_bf", align_bytes=64)
+        yw = [keep.tile([P, PACK, HALF], F32, name="yw%d" % h, tag="yw%d" % h, align_bytes=64) for h in range(2)]
+        g_rows = [
+            keep.tile([P, PACK, HALF], BF16, name="g_rows%d" % h, tag="g_rows%d" % h, align_bytes=64) for h in range(2)
+        ]
         g_bf = keep.tile([P, N, PACK], BF16, name="g_bf", align_bytes=64)
         xm_codes = keep.tile([P, D], U32, name="xm_codes", align_bytes=64)
         xm_scale = keep.tile([P, D], U8, name="xm_scale", align_bytes=64)
 
-        def weigh_a(h, tag):
-            aw.append(keep.tile([P, PACK, HALF], F32, name="aw%d" % h, tag=tag, align_bytes=64))
+        def weigh_y(h):
             for t in range(PACK):
-                nc.scalar.activation(
-                    aw[h][:, t, :], banks[t][:, h * HALF : (h + 1) * HALF], COPY, scale=weights[:, t : t + 1]
+                nc.scalar.activation(yw[h][:, t, :], y_raw[h][:, t, :], COPY, scale=weights[:, t : t + 1])
+
+        def form_g(h):
+            for t in range(PACK):
+                nc.vector.scalar_tensor_tensor(
+                    g_rows[h][:, t, :],
+                    banks[t][:, h * HALF : (h + 1) * HALF],
+                    weights[:, t : t + 1],
+                    yw[h][:, t, :],
+                    MULT,
+                    SUB,
                 )
 
-        def subtract(h):
-            cols = slice(h * HALF, (h + 1) * HALF)
-            nc.vector.tensor_tensor(
-                g_bf[:, cols, :].rearrange("p (c i) t -> p c t i", i=4),
-                aw[h][:].rearrange("p t (c i) -> p c t i", i=4),
-                yw[:, :, cols].rearrange("p t (c i) -> p c t i", i=4),
-                SUB,
+        def interleave(h, copy):
+            copy(
+                g_bf[:, h * HALF : (h + 1) * HALF, :].rearrange("p (c i) t -> p c t i", i=4),
+                g_rows[h][:].rearrange("p t (c i) -> p c t i", i=4),
             )
 
         def quantise_g(h):
@@ -196,29 +203,29 @@ def tile_attend_gsq_w_kernel(tc, xT, w_words, w_scales, y, wt, xm, offs, out):
             multiply(b, h * HALF, HALF, N, piece)
             return piece
 
-        for t in range(PACK):
-            nc.vector.tensor_scalar(yw[:, t, :], y_raw[t // 2][:, t % 2, :], weights[:, t : t + 1], None, MULT)
-        weigh_a(0, "aw0")
-        rounded0 = round_xm(0, 1, "xt_codes_then_xm")
-        weigh_a(1, "xm_raw0")
-        rounded1 = round_xm(1, 2, "weights_then_xm")
-        subtract(0)
+        weigh_y(0)
+        rounded0 = round_xm(0, 1, "xm_bf0")
+        rounded1 = round_xm(1, 2, "xm_bf1")
+        weigh_y(1)
+        form_g(0)
         quantise_xm(0, 1, rounded0[:])
-        quantise_g(0)
-        half00 = multiply_half(0, 0, "dense_then_xm")
-        subtract(1)
+        interleave(0, nc.vector.tensor_copy)
         quantise_xm(1, 2, rounded1[:])
+        quantise_g(0)
+        half00 = multiply_half(0, 0, "half00_then_xm")
+        form_g(1)
+        interleave(1, nc.scalar.copy)
+        half10 = multiply_half(1, 0, "g_rows1")
+        scatter(0, 0, HALF, half00)
         quantise_g(1)
-        half10 = multiply_half(1, 0, "half10")
+        rounded23 = round_xm(2, 4, "yw1")
         half01 = multiply_half(0, 1, "half01")
         half11 = multiply_half(1, 1, "half11")
-        rounded23 = round_xm(2, 4, "xm_raw0")
-        scatter(0, 0, HALF, half00)
         quantise_xm(2, 4, rounded23[:])
         scatter(1, 0, HALF, half10)
         scatter(0, HALF, N, half01)
         store(0)
-        late = round_xm(4, 8, "dense_then_xm")
+        late = round_xm(4, 8, "half00_then_xm")
         multiply_whole(2)
         scatter(1, HALF, N, half11)
         store(1)

@@ -23,10 +23,11 @@ PACK = 4
 PASSES = D // (P * PACK)
 BLOCKS = D // P
 WINDOWS = 3
-VECTOR_M = (76, 56)
+VECTOR_M = ((84, 0), (128, 40))
 HALF = N // 2
-XM_CHUNKS = ((0, 256), (256, 512), (512, 1024))
-QUANT_T = (2, 1)
+WORDS_FIRST = 512
+XT_PIECES = (((0, 4),), ((0, 2), (2, 4)))
+XM_CHUNKS = ((0, 128), (128, 256), (256, 512), (512, 1024))
 
 
 def tile_attend_gsq_w_kernel(tc, xT, w_words, w_scales, y, wt, xm, offs, out):
@@ -39,47 +40,72 @@ def tile_attend_gsq_w_kernel(tc, xT, w_words, w_scales, y, wt, xm, offs, out):
 
         offsets = keep.tile([P, N // 16], U16, name="offsets")
         word_table = keep.tile([P, T], I32, name="word_table", align_bytes=64)
-        scale_table = [keep.tile([P, T], U8, name="scale_table%d" % o, align_bytes=64) for o in range(PASSES)]
+        scale_table = keep.tile([P, T], U8, name="scale_table", align_bytes=64)
+        w_scale = [keep.tile([P, N], U8, name="w_scale%d" % o, align_bytes=64) for o in range(PASSES)]
         weights = keep.tile([P, PACK], F32, name="weights", align_bytes=64)
         xt_raw = [
-            keep.tile([P, PACK, R], F32, name="xt_raw%d" % o, tag="xt_raw%d" % o, align_bytes=64) for o in range(PASSES)
+            [keep.tile([P, hi - lo, R], F32, name="xt_raw%d%d" % (o, lo), align_bytes=64) for lo, hi in XT_PIECES[o]]
+            for o in range(PASSES)
         ]
-        y_raw = [keep.tile([P, PACK, HALF], F32, name="y_raw%d" % h, align_bytes=64) for h in range(2)]
+        y_raw = [
+            [keep.tile([P, 2, HALF], F32, name="y_raw%d%d" % (h, u), align_bytes=64) for u in range(2)] for h in range(2)
+        ]
         xm_raw = [
             keep.tile([P, PACK, hi - lo], F32, name="xm_raw%d" % lo, tag="xm_raw%d" % lo, align_bytes=64)
             for lo, hi in XM_CHUNKS
         ]
-        windows = [keep.tile([P, T], F32, name="window%d" % w, align_bytes=64) for w in range(WINDOWS)]
+        windows = [keep.tile([P, T], F32, name="window%d" % w, align_bytes=64) for w in range(WINDOWS - 1)]
 
-        for o in range(PASSES):
-            nc.vector.memset(scale_table[o][:].bitcast(I32), 0)
+        nc.vector.memset(scale_table[:].bitcast(I32), 0)
 
-        nc.sync.dma_start(word_table[:], w_words[0].rearrange("p t b -> p (t b)").bitcast(I32))
+        word_rows = w_words[0].rearrange("p t b -> p (t b)").bitcast(I32)
+        nc.sync.dma_start(word_table[:, :WORDS_FIRST], word_rows[:, :WORDS_FIRST])
         nc.sync.dma_start(offsets[:], offs)
-        for o in range(PASSES):
-            for s in range(4):
-                nc.sync.dma_start(scale_table[o][s:P:32, :].bitcast(I32), w_scales[o, s:16:4, :].bitcast(I32))
-            nc.sync.dma_start(xt_raw[o][:], xT[0, 512 * o : 512 * (o + 1), :].rearrange("(p j) r -> p j r", j=PACK))
-        nc.sync.dma_start(weights[:], wt[0].rearrange("(p t) one -> p (t one)", t=PACK))
-        y_rows = y[0].rearrange("(p t) i -> p t i", t=PACK)
-        xm_rows = xm[0].rearrange("(p t) d -> p t d", t=PACK)
-        for c, (lo, hi) in enumerate(XM_CHUNKS):
-            if c < 2:
-                nc.sync.dma_start(y_raw[c][:], y_rows[:, :, c * HALF : (c + 1) * HALF])
-            nc.sync.dma_start(xm_raw[c][:], xm_rows[:, :, lo:hi])
+        nc.sync.dma_start(scale_table[0:P:4, :].bitcast(I32), w_scales.rearrange("o f t -> (o f) t").bitcast(I32))
+        nc.sync.dma_start(word_table[:, WORDS_FIRST:], word_rows[:, WORDS_FIRST:])
+        xt_rows = [xT[0, 512 * o : 512 * (o + 1), :].rearrange("(p j) r -> p j r", j=PACK) for o in range(PASSES)]
+        nc.sync.dma_start(xt_raw[0][0][:], xt_rows[0])
 
         g_codes = keep.tile([P, HALF + N], U32, name="g_codes", align_bytes=64)
         g_scale = keep.tile([P, HALF + N], U8, name="g_scale", align_bytes=64)
+        for o in range(PASSES):
+            nc.vector.memset(w_scale[o][:].bitcast(I32), 0)
         nc.vector.memset(g_codes[:, :HALF].bitcast(I32), 0)
         nc.vector.memset(g_scale[:, :HALF].bitcast(I32), 0)
-        for w in range(WINDOWS):
-            nc.vector.memset(windows[w][:].bitcast(I32), 0)
+        nc.vector.memset(windows[0][:].bitcast(I32), 0)
+        nc.vector.memset(windows[1][:, : T // 2].bitcast(I32), 0)
 
+        scale_rows = keep.tile([P, N], U8, name="scale_rows", align_bytes=64)
+        nc.vector.tensor_copy(scale_rows[:], scale_table[:].indirect(offsets[:]))
         pair_words = keep.tile([P, N], U32, name="pair_words", align_bytes=64)
         nc.vector.tensor_copy(pair_words[:], word_table[:].bitcast(U32).indirect(offsets[:]))
 
-        w_scale = [keep.tile([P, N], U8, name="w_scale0", align_bytes=64)]
-        nc.vector.tensor_copy(w_scale[0][:], scale_table[0][:].indirect(offsets[:]))
+        nc.vector.memset(windows[1][:, T // 2 :].bitcast(I32), 0)
+
+        y_rows = y[0].rearrange("(p t) i -> p t i", t=PACK)
+        xm_rows = xm[0].rearrange("(p t) d -> p t d", t=PACK)
+
+        def move_scales(o):
+            for s in range(4):
+                rows = slice(64 * o + 4 * s, 64 * (o + 1), 16)
+                nc.sync.dma_start(w_scale[o][s:P:32, :].bitcast(I32), scale_rows[rows, :].bitcast(I32))
+
+        def load_y(h, u):
+            nc.sync.dma_start(y_raw[h][u][:], y_rows[:, 2 * u : 2 * u + 2, h * HALF : (h + 1) * HALF])
+
+        move_scales(0)
+        nc.sync.dma_start(weights[:], wt[0].rearrange("(p t) one -> p (t one)", t=PACK))
+        for k, (lo, hi) in enumerate(XT_PIECES[1]):
+            nc.sync.dma_start(xt_raw[1][k][:], xt_rows[1][:, lo:hi, :])
+        move_scales(1)
+        load_y(0, 0)
+        load_y(0, 1)
+        for c, (lo, hi) in enumerate(XM_CHUNKS):
+            nc.sync.dma_start(xm_raw[c][:], xm_rows[:, :, lo:hi])
+            if c == 0:
+                load_y(1, 0)
+                load_y(1, 1)
+
         w_codes = keep.tile([P, PASSES, 2 * N], U8, name="w_codes", align_bytes=64)
         halves = pair_words[:].bitcast(U16).rearrange("p (i o) -> p o i", o=PASSES)
         nc.vector.tensor_copy(w_codes[:, 0, :].bitcast(U16), halves[:, 0, :])
@@ -88,24 +114,27 @@ def tile_attend_gsq_w_kernel(tc, xT, w_words, w_scales, y, wt, xm, offs, out):
         xt_scale = keep.tile([P, PASSES, R], U8, name="xt_scale", align_bytes=64)
         banks = [psum_a.tile([P, N], F32, name="a%d" % t) for t in range(PACK)]
         for o in range(PASSES):
-            xt_bf = keep.tile([P, PACK, P, PACK], BF16, name="xt_bf%d" % o, tag="xt_bf", align_bytes=64)
-            src = xt_raw[o][:].rearrange("p j (m t) -> p m j t", t=PACK)
-            dst = xt_bf[:].rearrange("p t m j -> p m j t")
-            mv = VECTOR_M[o]
-            nc.scalar.copy(dst[:, mv:, :, :], src[:, mv:, :, :])
-            nc.vector.tensor_copy(dst[:, :mv, :, :], src[:, :mv, :, :])
+            xt_bf = [
+                keep.tile([P, 2, P, PACK], BF16, name="xt_bf%d%d" % (o, u), align_bytes=64)
+                for u in range(2)
+            ]
+            dst = [xt_bf[u][:].rearrange("p t m j -> p m j t") for u in range(2)]
+            for k, (lo, hi) in enumerate(XT_PIECES[o]):
+                src = xt_raw[o][k][:].rearrange("p j (m t) -> p m j t", t=PACK)
+                for u in range(2):
+                    mv = VECTOR_M[o][u]
+                    if mv < P:
+                        nc.scalar.copy(dst[u][:, mv:, lo:hi, :], src[:, mv:, :, 2 * u : 2 * u + 2])
+                    if mv:
+                        nc.vector.tensor_copy(dst[u][:, :mv, lo:hi, :], src[:, :mv, :, 2 * u : 2 * u + 2])
             if o == 0:
                 nc.vector.tensor_copy(w_codes[:, 1, :].bitcast(U16), halves[:, 1, :])
-            step = QUANT_T[o]
-            for t in range(0, PACK, step):
+            for t in range(PACK):
                 nc.vector.quantize_mx(
-                    out=xt_codes[:, o, P * t : P * (t + step)].bitcast(E4M3),
-                    scales=xt_scale[:, o, P * t : P * (t + step)],
-                    in_=xt_bf[:, t : t + step, :, :].rearrange("p t m j -> p (t m j)"),
+                    out=xt_codes[:, o, P * t : P * (t + 1)].bitcast(E4M3),
+                    scales=xt_scale[:, o, P * t : P * (t + 1)],
+                    in_=xt_bf[t // 2][:, t % 2, :, :].rearrange("p m j -> p (m j)"),
                 )
-            if o == 0:
-                w_scale.append(keep.tile([P, N], U8, name="w_scale1", tag="xt_raw0", align_bytes=64))
-                nc.vector.tensor_copy(w_scale[1][:], scale_table[1][:].indirect(offsets[:]))
             for t in range(PACK):
                 nc.tensor.matmul_mx(
                     out=banks[t][:],
@@ -121,29 +150,28 @@ def tile_attend_gsq_w_kernel(tc, xT, w_words, w_scales, y, wt, xm, offs, out):
         g_rows = [
             keep.tile([P, PACK, HALF], BF16, name="g_rows%d" % h, tag="g_rows%d" % h, align_bytes=64) for h in range(2)
         ]
-        g_bf = keep.tile([P, N, PACK], BF16, name="g_bf", align_bytes=64)
+        g_bf = [keep.tile([P, HALF, PACK], BF16, name="g_bf%d" % h, tag="g_bf%d" % h, align_bytes=64) for h in range(2)]
         xm_codes = keep.tile([P, D], U32, name="xm_codes", align_bytes=64)
         xm_scale = keep.tile([P, D], U8, name="xm_scale", align_bytes=64)
 
         def weigh_y(h):
             for t in range(PACK):
-                nc.scalar.activation(yw[h][:, t, :], y_raw[h][:, t, :], COPY, scale=weights[:, t : t + 1])
+                nc.scalar.activation(yw[h][:, t, :], y_raw[h][t // 2][:, t % 2, :], COPY, scale=weights[:, t : t + 1])
 
-        def form_g(h):
-            for t in range(PACK):
-                nc.vector.scalar_tensor_tensor(
-                    g_rows[h][:, t, :],
-                    banks[t][:, h * HALF : (h + 1) * HALF],
-                    weights[:, t : t + 1],
-                    yw[h][:, t, :],
-                    MULT,
-                    SUB,
-                )
+        def form_g(h, t, lo=0, hi=HALF):
+            nc.vector.scalar_tensor_tensor(
+                g_rows[h][:, t, lo:hi],
+                banks[t][:, h * HALF + lo : h * HALF + hi],
+                weights[:, t : t + 1],
+                yw[h][:, t, lo:hi],
+                MULT,
+                SUB,
+            )
 
-        def interleave(h, copy):
+        def interleave(h, copy, lo=0, hi=HALF):
             copy(
-                g_bf[:, h * HALF : (h + 1) * HALF, :].rearrange("p (c i) t -> p c t i", i=4),
-                g_rows[h][:].rearrange("p t (c i) -> p c t i", i=4),
+                g_bf[h][:, lo:hi, :].rearrange("p (c i) t -> p c t i", i=4),
+                g_rows[h][:, :, lo:hi].rearrange("p t (c i) -> p c t i", i=4),
             )
 
         def quantise_g(h):
@@ -151,7 +179,7 @@ def tile_attend_gsq_w_kernel(tc, xT, w_words, w_scales, y, wt, xm, offs, out):
             nc.vector.quantize_mx(
                 out=g_codes[:, cols].bitcast(E5M2),
                 scales=g_scale[:, cols],
-                in_=g_bf[:, h * HALF : (h + 1) * HALF, :].rearrange("p i t -> p (i t)"),
+                in_=g_bf[h][:].rearrange("p i t -> p (i t)"),
             )
 
         def round_xm(first, last, tag):
@@ -205,15 +233,20 @@ def tile_attend_gsq_w_kernel(tc, xT, w_words, w_scales, y, wt, xm, offs, out):
 
         weigh_y(0)
         rounded0 = round_xm(0, 1, "xm_bf0")
-        rounded1 = round_xm(1, 2, "xm_bf1")
         weigh_y(1)
-        form_g(0)
+        rounded1 = round_xm(1, 2, "xm_bf1")
+        for t in range(PACK - 1):
+            form_g(0, t)
+        form_g(0, PACK - 1, 0, HALF // 2)
+        form_g(0, PACK - 1, HALF // 2, HALF)
+        interleave(0, nc.vector.tensor_copy, 0, HALF // 2)
+        interleave(0, nc.vector.tensor_copy, HALF // 2, HALF)
         quantise_xm(0, 1, rounded0[:])
-        interleave(0, nc.vector.tensor_copy)
-        quantise_xm(1, 2, rounded1[:])
         quantise_g(0)
-        half00 = multiply_half(0, 0, "half00_then_xm")
-        form_g(1)
+        half00 = multiply_half(0, 0, "xm_raw128")
+        for t in range(PACK):
+            form_g(1, t)
+        quantise_xm(1, 2, rounded1[:])
         interleave(1, nc.scalar.copy)
         half10 = multiply_half(1, 0, "g_rows1")
         scatter(0, 0, HALF, half00)
@@ -222,10 +255,12 @@ def tile_attend_gsq_w_kernel(tc, xT, w_words, w_scales, y, wt, xm, offs, out):
         half01 = multiply_half(0, 1, "half01")
         half11 = multiply_half(1, 1, "half11")
         quantise_xm(2, 4, rounded23[:])
+        windows.append(keep.tile([P, T], F32, name="window2", tag="yw1", align_bytes=64))
+        nc.gpsimd.memset(windows[2][:].bitcast(I32), 0)
         scatter(1, 0, HALF, half10)
         scatter(0, HALF, N, half01)
         store(0)
-        late = round_xm(4, 8, "half00_then_xm")
+        late = round_xm(4, 8, "xm_raw128")
         multiply_whole(2)
         scatter(1, HALF, N, half11)
         store(1)

@@ -35,8 +35,7 @@ def tile_attend_gsq_w_kernel(tc, xT, w_words, w_scales, y, wt, xm, offs, out):
     with ExitStack() as ctx:
         keep = ctx.enter_context(tc.tile_pool(name="keep", bufs=1))
         ring = ctx.enter_context(tc.tile_pool(name="ring", bufs=3))
-        psum_a = ctx.enter_context(tc.psum_pool(name="psum_a", bufs=1))
-        psum_dw = ctx.enter_context(tc.psum_pool(name="psum_dw", bufs=4))
+        psum = ctx.enter_context(tc.psum_pool(name="psum", bufs=1))
 
         offsets = keep.tile([P, N // 16], U16, name="offsets")
         word_table = keep.tile([P, T], I32, name="word_table", align_bytes=64)
@@ -93,12 +92,12 @@ def tile_attend_gsq_w_kernel(tc, xT, w_words, w_scales, y, wt, xm, offs, out):
         def load_y(h, u):
             nc.sync.dma_start(y_raw[h][u][:], y_rows[:, 2 * u : 2 * u + 2, h * HALF : (h + 1) * HALF])
 
+        nc.sync.dma_start(xt_raw[1][0][:], xt_rows[1][:, :2, :])
         move_scales(0)
+        nc.sync.dma_start(xt_raw[1][1][:], xt_rows[1][:, 2:, :])
         nc.sync.dma_start(weights[:], wt[0].rearrange("(p t) one -> p (t one)", t=PACK))
-        for k, (lo, hi) in enumerate(XT_PIECES[1]):
-            nc.sync.dma_start(xt_raw[1][k][:], xt_rows[1][:, lo:hi, :])
-        move_scales(1)
         load_y(0, 0)
+        move_scales(1)
         load_y(0, 1)
         for c, (lo, hi) in enumerate(XM_CHUNKS):
             nc.sync.dma_start(xm_raw[c][:], xm_rows[:, :, lo:hi])
@@ -112,7 +111,22 @@ def tile_attend_gsq_w_kernel(tc, xT, w_words, w_scales, y, wt, xm, offs, out):
 
         xt_codes = keep.tile([P, PASSES, R], U32, name="xt_codes", align_bytes=64)
         xt_scale = keep.tile([P, PASSES, R], U8, name="xt_scale", align_bytes=64)
-        banks = [psum_a.tile([P, N], F32, name="a%d" % t) for t in range(PACK)]
+        banks = [[psum.tile([P, N], F32, name="a%d%d" % (q, t), tag="bank%d%d" % (q, t)) for t in range(PACK)] for q in range(2)]
+
+        def scores(q, t):
+            return banks[1][t][:, :P] if q == 1 else banks[0][t][:, P * max(q - 1, 0) : P * max(q, 1)]
+
+        def score_pass(o, q, t):
+            nc.tensor.matmul_mx(
+                out=scores(q, t),
+                lhsT=xt_codes[:, o, P * t : P * (t + 1)].bitcast(E4M3),
+                lhsT_scale=xt_scale[:, o, P * t : P * (t + 1)],
+                rhs=w_codes[:, o, 2 * P * q : 2 * P * (q + 1)].bitcast(E2M1),
+                rhs_scale=w_scale[o][:, P * q : P * (q + 1)],
+                start=(o == 0),
+                stop=(o == PASSES - 1),
+            )
+
         for o in range(PASSES):
             xt_bf = [
                 keep.tile([P, 2, P, PACK], BF16, name="xt_bf%d%d" % (o, u), align_bytes=64)
@@ -136,15 +150,8 @@ def tile_attend_gsq_w_kernel(tc, xT, w_words, w_scales, y, wt, xm, offs, out):
                     in_=xt_bf[t // 2][:, t % 2, :, :].rearrange("p m j -> p (m j)"),
                 )
             for t in range(PACK):
-                nc.tensor.matmul_mx(
-                    out=banks[t][:],
-                    lhsT=xt_codes[:, o, P * t : P * (t + 1)].bitcast(E4M3),
-                    lhsT_scale=xt_scale[:, o, P * t : P * (t + 1)],
-                    rhs=w_codes[:, o, :].bitcast(E2M1),
-                    rhs_scale=w_scale[o][:],
-                    start=(o == 0),
-                    stop=(o == PASSES - 1),
-                )
+                for q in range(2):
+                    score_pass(o, q, t)
 
         yw = [keep.tile([P, PACK, HALF], F32, name="yw%d" % h, tag="yw%d" % h, align_bytes=64) for h in range(2)]
         g_rows = [
@@ -161,7 +168,7 @@ def tile_attend_gsq_w_kernel(tc, xT, w_words, w_scales, y, wt, xm, offs, out):
         def form_g(h, t, lo=0, hi=HALF):
             nc.vector.scalar_tensor_tensor(
                 g_rows[h][:, t, lo:hi],
-                banks[t][:, h * HALF + lo : h * HALF + hi],
+                banks[0][t][:, P : P + HALF] if h else scores(lo // P, t),
                 weights[:, t : t + 1],
                 yw[h][:, t, lo:hi],
                 MULT,
@@ -201,8 +208,11 @@ def tile_attend_gsq_w_kernel(tc, xT, w_words, w_scales, y, wt, xm, offs, out):
                 in_=rounded.rearrange("p d t -> p (d t)"),
             )
 
+        products = []
+
         def multiply(b, start, lo, hi, piece):
-            acc = psum_dw.tile([P, N], F32, name="acc")
+            acc = psum.tile([P, N], F32, name="acc", tag="bank1%d" % (len(products) % PACK))
+            products.append(b)
             nc.tensor.matmul_mx(
                 out=acc[:],
                 lhsT=xm_codes[:, b * P : (b + 1) * P].bitcast(E4M3),
@@ -235,10 +245,13 @@ def tile_attend_gsq_w_kernel(tc, xT, w_words, w_scales, y, wt, xm, offs, out):
         rounded0 = round_xm(0, 1, "xm_bf0")
         weigh_y(1)
         rounded1 = round_xm(1, 2, "xm_bf1")
-        for t in range(PACK - 1):
-            form_g(0, t)
-        form_g(0, PACK - 1, 0, HALF // 2)
-        form_g(0, PACK - 1, HALF // 2, HALF)
+        for t in range(PACK):
+            form_g(0, t, 0, P)
+            form_g(0, t, P, HALF)
+        for t in range(PACK):
+            for q in range(2, 4):
+                for o in range(PASSES):
+                    score_pass(o, q, t)
         interleave(0, nc.vector.tensor_copy, 0, HALF // 2)
         interleave(0, nc.vector.tensor_copy, HALF // 2, HALF)
         quantise_xm(0, 1, rounded0[:])

@@ -25,7 +25,7 @@ BLOCKS = D // P
 WINDOWS = 3
 VECTOR_M = ((84, 0), (128, 40))
 HALF = N // 2
-WORDS_FIRST = 512
+WORDS_FIRST = 768
 XT_PIECES = (((0, 4),), ((0, 2), (2, 4)))
 XM_CHUNKS = ((0, 128), (128, 256), (256, 512), (512, 1024))
 

@@ -69,17 +69,16 @@ def tile_attend_gsq_w_kernel(tc, xT, w_words, w_scales, y, wt, xm, offs, out):
         g_scale = keep.tile([P, HALF + N], U8, name="g_scale", align_bytes=64)
         for o in range(PASSES):
             nc.vector.memset(w_scale[o][:].bitcast(I32), 0)
-        nc.vector.memset(g_codes[:, :HALF].bitcast(I32), 0)
-        nc.vector.memset(g_scale[:, :HALF].bitcast(I32), 0)
-        nc.vector.memset(windows[0][:].bitcast(I32), 0)
-        nc.vector.memset(windows[1][:, : T // 2].bitcast(I32), 0)
+        for window in windows:
+            nc.vector.memset(window[:].bitcast(I32), 0)
 
         scale_rows = keep.tile([P, N], U8, name="scale_rows", align_bytes=64)
         nc.vector.tensor_copy(scale_rows[:], scale_table[:].indirect(offsets[:]))
         pair_words = keep.tile([P, N], U32, name="pair_words", align_bytes=64)
         nc.vector.tensor_copy(pair_words[:], word_table[:].bitcast(U32).indirect(offsets[:]))
 
-        nc.vector.memset(windows[1][:, T // 2 :].bitcast(I32), 0)
+        nc.vector.memset(g_codes[:, :HALF].bitcast(I32), 0)
+        nc.vector.memset(g_scale[:, :HALF].bitcast(I32), 0)
 
         y_rows = y[0].rearrange("(p t) i -> p t i", t=PACK)
         xm_rows = xm[0].rearrange("(p t) d -> p t d", t=PACK)

@@ -25,9 +25,12 @@ BLOCKS = D // P
 WINDOWS = 3
 VECTOR_M = ((84, 0), (128, 40))
 HALF = N // 2
+SCALAR_SLOTS = 160
+VECTOR_SLOTS = 160
+PRODUCT_BANKS = ("bank7", "bank4", "bank0", "bank1")
 WORDS_FIRST = 768
 XT_PIECES = (((0, 4),), ((0, 2), (2, 4)))
-XM_CHUNKS = ((0, 128), (128, 256), (256, 512), (512, 1024))
+XM_CHUNKS = tuple((lo, lo + P) for lo in range(0, D, P))
 
 
 def tile_attend_gsq_w_kernel(tc, xT, w_words, w_scales, y, wt, xm, offs, out):
@@ -40,7 +43,7 @@ def tile_attend_gsq_w_kernel(tc, xT, w_words, w_scales, y, wt, xm, offs, out):
         offsets = keep.tile([P, N // 16], U16, name="offsets")
         word_table = keep.tile([P, T], I32, name="word_table", align_bytes=64)
         scale_table = keep.tile([P, T], U8, name="scale_table", align_bytes=64)
-        w_scale = [keep.tile([P, N], U8, name="w_scale%d" % o, align_bytes=64) for o in range(PASSES)]
+        w_scale = keep.tile([P, PASSES, N], U8, name="w_scale", align_bytes=64)
         weights = keep.tile([P, PACK], F32, name="weights", align_bytes=64)
         xt_raw = [
             [keep.tile([P, hi - lo, R], F32, name="xt_raw%d%d" % (o, lo), align_bytes=64) for lo, hi in XT_PIECES[o]]
@@ -60,15 +63,15 @@ def tile_attend_gsq_w_kernel(tc, xT, w_words, w_scales, y, wt, xm, offs, out):
         word_rows = w_words[0].rearrange("p t b -> p (t b)").bitcast(I32)
         nc.sync.dma_start(word_table[:, :WORDS_FIRST], word_rows[:, :WORDS_FIRST])
         nc.sync.dma_start(offsets[:], offs)
-        nc.sync.dma_start(scale_table[0:P:4, :].bitcast(I32), w_scales.rearrange("o f t -> (o f) t").bitcast(I32))
+        nc.sync.dma_start(scale_table[0:P:4, :].bitcast(I32), w_scales.bitcast(I32).rearrange("o f w -> f o w"))
         nc.sync.dma_start(word_table[:, WORDS_FIRST:], word_rows[:, WORDS_FIRST:])
         xt_rows = [xT[0, 512 * o : 512 * (o + 1), :].rearrange("(p j) r -> p j r", j=PACK) for o in range(PASSES)]
         nc.sync.dma_start(xt_raw[0][0][:], xt_rows[0])
 
         g_codes = keep.tile([P, HALF + N], U32, name="g_codes", align_bytes=64)
         g_scale = keep.tile([P, HALF + N], U8, name="g_scale", align_bytes=64)
-        for o in range(PASSES):
-            nc.vector.memset(w_scale[o][:].bitcast(I32), 0)
+        planes = w_scale[:].rearrange("p o i -> p (o i)").bitcast(I32)
+        nc.vector.memset(planes, 0)
         for window in windows:
             nc.vector.memset(window[:].bitcast(I32), 0)
 
@@ -83,24 +86,19 @@ def tile_attend_gsq_w_kernel(tc, xT, w_words, w_scales, y, wt, xm, offs, out):
         y_rows = y[0].rearrange("(p t) i -> p t i", t=PACK)
         xm_rows = xm[0].rearrange("(p t) d -> p t d", t=PACK)
 
-        def move_scales(o):
-            for s in range(4):
-                rows = slice(64 * o + 4 * s, 64 * (o + 1), 16)
-                nc.sync.dma_start(w_scale[o][s:P:32, :].bitcast(I32), scale_rows[rows, :].bitcast(I32))
-
         def load_y(h, u):
             nc.sync.dma_start(y_raw[h][u][:], y_rows[:, 2 * u : 2 * u + 2, h * HALF : (h + 1) * HALF])
 
         nc.sync.dma_start(xt_raw[1][0][:], xt_rows[1][:, :2, :])
-        move_scales(0)
+        for q in range(0, P, 32):
+            nc.sync.dma_start(planes[q : q + 4, :], scale_rows[q : q + 32 : 4, :].bitcast(I32))
         nc.sync.dma_start(xt_raw[1][1][:], xt_rows[1][:, 2:, :])
         nc.sync.dma_start(weights[:], wt[0].rearrange("(p t) one -> p (t one)", t=PACK))
         load_y(0, 0)
-        move_scales(1)
         load_y(0, 1)
         for c, (lo, hi) in enumerate(XM_CHUNKS):
             nc.sync.dma_start(xm_raw[c][:], xm_rows[:, :, lo:hi])
-            if c == 0:
+            if c == 1:
                 load_y(1, 0)
                 load_y(1, 1)
 
@@ -110,10 +108,14 @@ def tile_attend_gsq_w_kernel(tc, xT, w_words, w_scales, y, wt, xm, offs, out):
 
         xt_codes = keep.tile([P, PASSES, R], U32, name="xt_codes", align_bytes=64)
         xt_scale = keep.tile([P, PASSES, R], U8, name="xt_scale", align_bytes=64)
-        banks = [[psum.tile([P, N], F32, name="a%d%d" % (q, t), tag="bank%d%d" % (q, t)) for t in range(PACK)] for q in range(2)]
+        banks = [psum.tile([P, N], F32, name="a%d" % t, tag="bank%d" % t) for t in range(PACK)]
+        side_bank = psum.tile([P, N], F32, name="a_side", tag="bank4")
+        pairs = [psum.tile([P, 2, HALF], F32, name="a_pair%d" % u, tag="bank%d" % (5 + u)) for u in range(2)]
 
         def scores(q, t):
-            return banks[1][t][:, :P] if q == 1 else banks[0][t][:, P * max(q - 1, 0) : P * max(q, 1)]
+            if q >= 2:
+                return pairs[t // 2][:, t % 2, P * (q - 2) : P * (q - 1)]
+            return (side_bank if (q, t) == (1, 0) else banks[t])[:, P * q : P * (q + 1)]
 
         def score_pass(o, q, t):
             nc.tensor.matmul_mx(
@@ -121,9 +123,9 @@ def tile_attend_gsq_w_kernel(tc, xT, w_words, w_scales, y, wt, xm, offs, out):
                 lhsT=xt_codes[:, o, P * t : P * (t + 1)].bitcast(E4M3),
                 lhsT_scale=xt_scale[:, o, P * t : P * (t + 1)],
                 rhs=w_codes[:, o, 2 * P * q : 2 * P * (q + 1)].bitcast(E2M1),
-                rhs_scale=w_scale[o][:, P * q : P * (q + 1)],
-                start=(o == 0),
-                stop=(o == PASSES - 1),
+                rhs_scale=w_scale[:, o, P * q : P * (q + 1)],
+                start=(o == 0 and ((q, t % 2) == (2, 0) if q >= 2 else (q == 0 or t == 0))),
+                stop=(o == PASSES - 1 and ((q, t % 2) == (3, 1) if q >= 2 else (q == 1 or t == 0))),
             )
 
         for o in range(PASSES):
@@ -152,33 +154,26 @@ def tile_attend_gsq_w_kernel(tc, xT, w_words, w_scales, y, wt, xm, offs, out):
                 for q in range(2):
                     score_pass(o, q, t)
 
-        yw = [keep.tile([P, PACK, HALF], F32, name="yw%d" % h, tag="yw%d" % h, align_bytes=64) for h in range(2)]
-        g_rows = [
-            keep.tile([P, PACK, HALF], BF16, name="g_rows%d" % h, tag="g_rows%d" % h, align_bytes=64) for h in range(2)
-        ]
+        yw = keep.tile([P, PACK, HALF], F32, name="yw", align_bytes=64)
+        g_rows = keep.tile([P, PACK, HALF], BF16, name="g_rows", tag="g_rows", align_bytes=64)
+        late_rows = keep.tile([P, PACK, SCALAR_SLOTS], BF16, name="late_rows", align_bytes=64)
+        residual = keep.tile([P, PACK, HALF], F32, name="residual", tag="residual", align_bytes=64)
         g_bf = [keep.tile([P, HALF, PACK], BF16, name="g_bf%d" % h, tag="g_bf%d" % h, align_bytes=64) for h in range(2)]
         xm_codes = keep.tile([P, D], U32, name="xm_codes", align_bytes=64)
         xm_scale = keep.tile([P, D], U8, name="xm_scale", align_bytes=64)
 
-        def weigh_y(h):
-            for t in range(PACK):
-                nc.scalar.activation(yw[h][:, t, :], y_raw[h][t // 2][:, t % 2, :], COPY, scale=weights[:, t : t + 1])
-
-        def form_g(h, t, lo=0, hi=HALF):
+        def form_g(t, lo=0, hi=HALF):
             nc.vector.scalar_tensor_tensor(
-                g_rows[h][:, t, lo:hi],
-                banks[0][t][:, P : P + HALF] if h else scores(lo // P, t),
+                g_rows[:, t, lo:hi],
+                scores(1, 0) if (t, lo) == (0, P) else banks[t][:, lo:hi],
                 weights[:, t : t + 1],
-                yw[h][:, t, lo:hi],
+                yw[:, t, lo:hi],
                 MULT,
                 SUB,
             )
 
-        def interleave(h, copy, lo=0, hi=HALF):
-            copy(
-                g_bf[h][:, lo:hi, :].rearrange("p (c i) t -> p c t i", i=4),
-                g_rows[h][:, :, lo:hi].rearrange("p t (c i) -> p c t i", i=4),
-            )
+        def interleave(copy, woven, rows):
+            copy(woven.rearrange("p (c i) t -> p c t i", i=4), rows.rearrange("p t (c i) -> p c t i", i=4))
 
         def quantise_g(h):
             cols = slice((h + 1) * HALF, (h + 2) * HALF)
@@ -210,7 +205,7 @@ def tile_attend_gsq_w_kernel(tc, xT, w_words, w_scales, y, wt, xm, offs, out):
         products = []
 
         def multiply(b, start, lo, hi, piece):
-            acc = psum.tile([P, N], F32, name="acc", tag="bank1%d" % (len(products) % PACK))
+            acc = psum.tile([P, N], F32, name="acc", tag=PRODUCT_BANKS[len(products) % PACK])
             products.append(b)
             nc.tensor.matmul_mx(
                 out=acc[:],
@@ -240,39 +235,58 @@ def tile_attend_gsq_w_kernel(tc, xT, w_words, w_scales, y, wt, xm, offs, out):
             multiply(b, h * HALF, HALF, N, piece)
             return piece
 
-        weigh_y(0)
-        rounded0 = round_xm(0, 1, "xm_bf0")
-        weigh_y(1)
-        rounded1 = round_xm(1, 2, "xm_bf1")
         for t in range(PACK):
-            form_g(0, t, 0, P)
-            form_g(0, t, P, HALF)
+            nc.scalar.activation(yw[:, t, :], y_raw[0][t // 2][:, t % 2, :], COPY, scale=weights[:, t : t + 1])
+        rounded0 = round_xm(0, 1, "xm_bf0")
+        for t in range(PACK):
+            if 0 < t < PACK - 1:
+                form_g(t)
+            else:
+                form_g(t, 0, P)
+                form_g(t, P, HALF)
         for t in range(PACK):
             for q in range(2, 4):
                 for o in range(PASSES):
                     score_pass(o, q, t)
-        interleave(0, nc.vector.tensor_copy, 0, HALF // 2)
-        interleave(0, nc.vector.tensor_copy, HALF // 2, HALF)
+        for copy, lo, hi in (
+            (nc.scalar.copy, VECTOR_SLOTS, HALF),
+            (nc.vector.tensor_copy, 0, P),
+            (nc.vector.tensor_copy, P, VECTOR_SLOTS),
+        ):
+            interleave(copy, g_bf[0][:, lo:hi, :], g_rows[:, :, lo:hi])
+        rounded1 = round_xm(1, 2, "g_rows")
         quantise_xm(0, 1, rounded0[:])
         quantise_g(0)
-        half00 = multiply_half(0, 0, "xm_raw128")
+        half00 = multiply_half(0, 0, "half00")
+        for lo, hi in ((0, SCALAR_SLOTS), (SCALAR_SLOTS, HALF)):
+            for u in range(2):
+                nc.vector.tensor_tensor(
+                    residual[:, 2 * u : 2 * u + 2, lo:hi], pairs[u][:, :, lo:hi], y_raw[1][u][:, :, lo:hi], SUB
+                )
+            if lo == 0:
+                quantise_xm(1, 2, rounded1[:])
         for t in range(PACK):
-            form_g(1, t)
-        quantise_xm(1, 2, rounded1[:])
-        interleave(1, nc.scalar.copy)
-        half10 = multiply_half(1, 0, "g_rows1")
+            nc.scalar.activation(late_rows[:, t, :], residual[:, t, :SCALAR_SLOTS], COPY, scale=weights[:, t : t + 1])
+        interleave(nc.scalar.copy, g_bf[1][:, :SCALAR_SLOTS, :], late_rows[:])
+        nc.gpsimd.tensor_tensor(
+            g_bf[1][:, SCALAR_SLOTS:, :],
+            residual[:, :, SCALAR_SLOTS:].rearrange("p t i -> p i t"),
+            weights[:].unsqueeze(1).to_broadcast([P, HALF - SCALAR_SLOTS, PACK]),
+            MULT,
+        )
+        half10 = multiply_half(1, 0, "residual")
         scatter(0, 0, HALF, half00)
         quantise_g(1)
-        rounded23 = round_xm(2, 4, "yw1")
+        rounded23 = round_xm(2, 4, "g_bf1")
         half01 = multiply_half(0, 1, "half01")
         half11 = multiply_half(1, 1, "half11")
         quantise_xm(2, 4, rounded23[:])
-        windows.append(keep.tile([P, T], F32, name="window2", tag="yw1", align_bytes=64))
+        windows.append(keep.tile([P, T], F32, name="window2", tag="g_bf1", align_bytes=64))
         nc.gpsimd.memset(windows[2][:].bitcast(I32), 0)
         scatter(1, 0, HALF, half10)
         scatter(0, HALF, N, half01)
         store(0)
-        late = round_xm(4, 8, "xm_raw128")
+        late = round_xm(4, 8, "xm_raw384")
         multiply_whole(2)
         scatter(1, HALF, N, half11)
         store(1)

@@ -22,278 +22,289 @@ P = 128
 PACK = 4
 PASSES = D // (P * PACK)
 BLOCKS = D // P
-WINDOWS = 3
-VECTOR_M = ((84, 0), (128, 40))
 HALF = N // 2
-SCALAR_SLOTS = 160
-VECTOR_SLOTS = 160
-PRODUCT_BANKS = ("bank7", "bank4", "bank0", "bank1")
+WINDOWS = 4
+XT_LOADS = ((0, 0, R), (1, 0, R // 2), (1, R // 2, R))
+VECTOR_M = ((0, 0), (0, 0), (64, 12))
+PLACES = {
+    "window3": 0,
+    "scale_table": 0,
+    "xt_bf11": 18432,
+    "w_codes1": 18432,
+    "g_bf1": 8192,
+    "xm_bf3": 8192,
+    "xm_codes2": 9216,
+    "xm_bf4": 8192,
+    "xm_bf5": 8192,
+    "piece4_0": 12288,
+    "piece6_0": 12288,
+    "xm_raw2": 14336,
+    "piece0_0": 14336,
+}
 WORDS_FIRST = 768
-XT_PIECES = (((0, 4),), ((0, 2), (2, 4)))
-XM_CHUNKS = tuple((lo, lo + P) for lo in range(0, D, P))
+XM_LOADS = tuple((b, b + 1) for b in range(BLOCKS))
 
 
 def tile_attend_gsq_w_kernel(tc, xT, w_words, w_scales, y, wt, xm, offs, out):
     nc = tc.nc
     with ExitStack() as ctx:
         keep = ctx.enter_context(tc.tile_pool(name="keep", bufs=1))
-        ring = ctx.enter_context(tc.tile_pool(name="ring", bufs=3))
+        shared = ctx.enter_context(tc.tile_pool(name="shared", bufs=1))
         psum = ctx.enter_context(tc.psum_pool(name="psum", bufs=1))
 
+        def tile(shape, dtype, name, tag=None):
+            if name in PLACES:
+                return shared.tile(shape, dtype, name=name, align_bytes=64, offset=PLACES[name])
+            return keep.tile(shape, dtype, name=name, tag=tag or name, align_bytes=64)
+
         offsets = keep.tile([P, N // 16], U16, name="offsets")
-        word_table = keep.tile([P, T], I32, name="word_table", align_bytes=64)
-        scale_table = keep.tile([P, T], U8, name="scale_table", align_bytes=64)
-        w_scale = keep.tile([P, PASSES, N], U8, name="w_scale", align_bytes=64)
-        weights = keep.tile([P, PACK], F32, name="weights", align_bytes=64)
-        xt_raw = [
-            [keep.tile([P, hi - lo, R], F32, name="xt_raw%d%d" % (o, lo), align_bytes=64) for lo, hi in XT_PIECES[o]]
-            for o in range(PASSES)
-        ]
-        y_raw = [
-            [keep.tile([P, 2, HALF], F32, name="y_raw%d%d" % (h, u), align_bytes=64) for u in range(2)] for h in range(2)
-        ]
-        xm_raw = [
-            keep.tile([P, PACK, hi - lo], F32, name="xm_raw%d" % lo, tag="xm_raw%d" % lo, align_bytes=64)
-            for lo, hi in XM_CHUNKS
-        ]
-        windows = [keep.tile([P, T], F32, name="window%d" % w, align_bytes=64) for w in range(WINDOWS - 1)]
+        word_table = tile([P, T], I32, "word_table")
+        scale_table = tile([P, T], U8, "scale_table")
+        w_scale = tile([P, PASSES, N], U8, "w_scale")
+        weights = tile([P, PACK], F32, "weights")
+        xt_raw = [tile([P, PACK, hi - lo], F32, "xt_raw%d_%d" % (o, lo)) for o, lo, hi in XT_LOADS]
+        y_raw = [[tile([P, 2, HALF], F32, "y_raw%d%d" % (h, u)) for u in range(2)] for h in range(2)]
+        xm_raw = [tile([P, PACK, (hi - lo) * P], F32, "xm_raw%d" % lo) for lo, hi in XM_LOADS]
+        windows = [tile([P, T], F32, "window%d" % w) for w in range(WINDOWS - 1)]
 
         nc.vector.memset(scale_table[:].bitcast(I32), 0)
+
+        xt_rows = [xT[0, 512 * o : 512 * (o + 1), :].rearrange("(p j) r -> p j r", j=PACK) for o in range(PASSES)]
+
+        def load_xt(k):
+            o, lo, hi = XT_LOADS[k]
+            nc.sync.dma_start(xt_raw[k][:], xt_rows[o][:, :, lo:hi])
 
         word_rows = w_words[0].rearrange("p t b -> p (t b)").bitcast(I32)
         nc.sync.dma_start(word_table[:, :WORDS_FIRST], word_rows[:, :WORDS_FIRST])
         nc.sync.dma_start(offsets[:], offs)
         nc.sync.dma_start(scale_table[0:P:4, :].bitcast(I32), w_scales.bitcast(I32).rearrange("o f w -> f o w"))
+        load_xt(0)
         nc.sync.dma_start(word_table[:, WORDS_FIRST:], word_rows[:, WORDS_FIRST:])
-        xt_rows = [xT[0, 512 * o : 512 * (o + 1), :].rearrange("(p j) r -> p j r", j=PACK) for o in range(PASSES)]
-        nc.sync.dma_start(xt_raw[0][0][:], xt_rows[0])
 
-        g_codes = keep.tile([P, HALF + N], U32, name="g_codes", align_bytes=64)
-        g_scale = keep.tile([P, HALF + N], U8, name="g_scale", align_bytes=64)
         planes = w_scale[:].rearrange("p o i -> p (o i)").bitcast(I32)
         nc.vector.memset(planes, 0)
         for window in windows:
             nc.vector.memset(window[:].bitcast(I32), 0)
 
-        scale_rows = keep.tile([P, N], U8, name="scale_rows", align_bytes=64)
+        scale_rows = tile([P, N], U8, "scale_rows")
         nc.vector.tensor_copy(scale_rows[:], scale_table[:].indirect(offsets[:]))
-        pair_words = keep.tile([P, N], U32, name="pair_words", align_bytes=64)
-        nc.vector.tensor_copy(pair_words[:], word_table[:].bitcast(U32).indirect(offsets[:]))
-
-        nc.vector.memset(g_codes[:, :HALF].bitcast(I32), 0)
-        nc.vector.memset(g_scale[:, :HALF].bitcast(I32), 0)
+        windows.append(tile([P, T], F32, "window3"))
+        for window in windows[3:]:
+            nc.vector.memset(window[:].bitcast(I32), 0)
 
         y_rows = y[0].rearrange("(p t) i -> p t i", t=PACK)
         xm_rows = xm[0].rearrange("(p t) d -> p t d", t=PACK)
 
-        def load_y(h, u):
-            nc.sync.dma_start(y_raw[h][u][:], y_rows[:, 2 * u : 2 * u + 2, h * HALF : (h + 1) * HALF])
+        def load_y(h):
+            for u in range(2):
+                nc.sync.dma_start(y_raw[h][u][:], y_rows[:, 2 * u : 2 * u + 2, h * HALF : (h + 1) * HALF])
 
-        nc.sync.dma_start(xt_raw[1][0][:], xt_rows[1][:, :2, :])
+        load_xt(1)
         for q in range(0, P, 32):
             nc.sync.dma_start(planes[q : q + 4, :], scale_rows[q : q + 32 : 4, :].bitcast(I32))
-        nc.sync.dma_start(xt_raw[1][1][:], xt_rows[1][:, 2:, :])
+        load_xt(2)
         nc.sync.dma_start(weights[:], wt[0].rearrange("(p t) one -> p (t one)", t=PACK))
-        load_y(0, 0)
-        load_y(0, 1)
-        for c, (lo, hi) in enumerate(XM_CHUNKS):
-            nc.sync.dma_start(xm_raw[c][:], xm_rows[:, :, lo:hi])
-            if c == 1:
-                load_y(1, 0)
-                load_y(1, 1)
+        for c, (lo, hi) in enumerate(XM_LOADS):
+            if c < 2:
+                load_y(c)
+            nc.sync.dma_start(xm_raw[c][:], xm_rows[:, :, lo * P : hi * P])
 
-        w_codes = keep.tile([P, PASSES, 2 * N], U8, name="w_codes", align_bytes=64)
-        halves = pair_words[:].bitcast(U16).rearrange("p (i o) -> p o i", o=PASSES)
-        nc.vector.tensor_copy(w_codes[:, 0, :].bitcast(U16), halves[:, 0, :])
+        pair_words = tile([P, N], U32, "pair_words")
+        w_codes = {}
+        xt_codes = tile([P, PASSES, R], U32, "xt_codes")
+        xt_scale = tile([P, PASSES, R], U8, "xt_scale")
+        xt_bf = [[tile([P, 2, P, PACK], BF16, "xt_bf%d%d" % (o, u)) for u in range(2)] for o in range(PASSES)]
+        scores = {}
 
-        xt_codes = keep.tile([P, PASSES, R], U32, name="xt_codes", align_bytes=64)
-        xt_scale = keep.tile([P, PASSES, R], U8, name="xt_scale", align_bytes=64)
-        banks = [psum.tile([P, N], F32, name="a%d" % t, tag="bank%d" % t) for t in range(PACK)]
-        side_bank = psum.tile([P, N], F32, name="a_side", tag="bank4")
-        pairs = [psum.tile([P, 2, HALF], F32, name="a_pair%d" % u, tag="bank%d" % (5 + u)) for u in range(2)]
+        def round_xt(k):
+            o, lo, hi = XT_LOADS[k]
+            src = xt_raw[k][:].rearrange("p j (m t) -> p m j t", t=PACK)
+            for u in range(2):
+                dst = xt_bf[o][u][:].rearrange("p t m j -> p m j t")[:, lo // PACK : hi // PACK, :, :]
+                mv = VECTOR_M[k][u]
+                if mv < (hi - lo) // PACK:
+                    nc.scalar.copy(dst[:, mv:, :, :], src[:, mv:, :, 2 * u : 2 * u + 2])
+                if mv:
+                    nc.vector.tensor_copy(dst[:, :mv, :, :], src[:, :mv, :, 2 * u : 2 * u + 2])
 
-        def scores(q, t):
-            if q >= 2:
-                return pairs[t // 2][:, t % 2, P * (q - 2) : P * (q - 1)]
-            return (side_bank if (q, t) == (1, 0) else banks[t])[:, P * q : P * (q + 1)]
-
-        def score_pass(o, q, t):
-            nc.tensor.matmul_mx(
-                out=scores(q, t),
-                lhsT=xt_codes[:, o, P * t : P * (t + 1)].bitcast(E4M3),
-                lhsT_scale=xt_scale[:, o, P * t : P * (t + 1)],
-                rhs=w_codes[:, o, 2 * P * q : 2 * P * (q + 1)].bitcast(E2M1),
-                rhs_scale=w_scale[:, o, P * q : P * (q + 1)],
-                start=(o == 0 and ((q, t % 2) == (2, 0) if q >= 2 else (q == 0 or t == 0))),
-                stop=(o == PASSES - 1 and ((q, t % 2) == (3, 1) if q >= 2 else (q == 1 or t == 0))),
+        def quantise_xt(o, t):
+            nc.vector.quantize_mx(
+                out=xt_codes[:, o, P * t : P * (t + 1)].bitcast(E4M3),
+                scales=xt_scale[:, o, P * t : P * (t + 1)],
+                in_=xt_bf[o][t // 2][:, t % 2, :, :].rearrange("p m j -> p (m j)"),
             )
 
-        for o in range(PASSES):
-            xt_bf = [
-                keep.tile([P, 2, P, PACK], BF16, name="xt_bf%d%d" % (o, u), align_bytes=64)
-                for u in range(2)
-            ]
-            dst = [xt_bf[u][:].rearrange("p t m j -> p m j t") for u in range(2)]
-            for k, (lo, hi) in enumerate(XT_PIECES[o]):
-                src = xt_raw[o][k][:].rearrange("p j (m t) -> p m j t", t=PACK)
-                for u in range(2):
-                    mv = VECTOR_M[o][u]
-                    if mv < P:
-                        nc.scalar.copy(dst[u][:, mv:, lo:hi, :], src[:, mv:, :, 2 * u : 2 * u + 2])
-                    if mv:
-                        nc.vector.tensor_copy(dst[u][:, :mv, lo:hi, :], src[:, :mv, :, 2 * u : 2 * u + 2])
+        def score(o, h, t):
             if o == 0:
-                nc.vector.tensor_copy(w_codes[:, 1, :].bitcast(U16), halves[:, 1, :])
-            for t in range(PACK):
-                nc.vector.quantize_mx(
-                    out=xt_codes[:, o, P * t : P * (t + 1)].bitcast(E4M3),
-                    scales=xt_scale[:, o, P * t : P * (t + 1)],
-                    in_=xt_bf[t // 2][:, t % 2, :, :].rearrange("p m j -> p (m j)"),
-                )
-            for t in range(PACK):
-                for q in range(2):
-                    score_pass(o, q, t)
+                scores[h, t] = psum.tile([P, HALF], F32, name="scores", tag="bank%d" % t)
+            nc.tensor.matmul_mx(
+                out=scores[h, t][:],
+                lhsT=xt_codes[:, o, P * t : P * (t + 1)].bitcast(E4M3),
+                lhsT_scale=xt_scale[:, o, P * t : P * (t + 1)],
+                rhs=w_codes[h][:, o, :].bitcast(E2M1),
+                rhs_scale=w_scale[:, o, HALF * h : HALF * (h + 1)],
+                start=(o == 0),
+                stop=(o == PASSES - 1),
+            )
 
-        yw = keep.tile([P, PACK, HALF], F32, name="yw", align_bytes=64)
-        g_rows = keep.tile([P, PACK, HALF], BF16, name="g_rows", tag="g_rows", align_bytes=64)
-        late_rows = keep.tile([P, PACK, SCALAR_SLOTS], BF16, name="late_rows", align_bytes=64)
-        residual = keep.tile([P, PACK, HALF], F32, name="residual", tag="residual", align_bytes=64)
-        g_bf = [keep.tile([P, HALF, PACK], BF16, name="g_bf%d" % h, tag="g_bf%d" % h, align_bytes=64) for h in range(2)]
-        xm_codes = keep.tile([P, D], U32, name="xm_codes", align_bytes=64)
-        xm_scale = keep.tile([P, D], U8, name="xm_scale", align_bytes=64)
+        def split(h):
+            w_codes[h] = tile([P, PASSES, 2 * HALF], U8, "w_codes%d" % h)
+            by_pass = pair_words[:, h * HALF : (h + 1) * HALF].bitcast(U16).rearrange("p (i o) -> p o i", o=PASSES)
+            nc.vector.tensor_copy(w_codes[h][:].bitcast(U16), by_pass)
 
-        def form_g(t, lo=0, hi=HALF):
+        round_xt(0)
+        for t in range(2):
+            quantise_xt(0, t)
+        nc.vector.tensor_copy(pair_words[:], word_table[:].bitcast(U32).indirect(offsets[:]))
+        split(0)
+        for t in range(PACK):
+            if t >= 2:
+                quantise_xt(0, t)
+            score(0, 0, t)
+        round_xt(1)
+        round_xt(2)
+        for t in range(PACK):
+            quantise_xt(1, t)
+            score(1, 0, t)
+        split(1)
+
+        yw = {}
+        g_rows = [tile([P, PACK, HALF], BF16, "g_rows%d" % h) for h in range(2)]
+        g_bf = [tile([P, HALF, PACK], BF16, "g_bf%d" % h) for h in range(2)]
+        g_codes = tile([P, N], U32, "g_codes")
+        g_scale = tile([P, N], U8, "g_scale")
+        xm_codes = {}
+        xm_scale = tile([P, D], U8, "xm_scale")
+
+        def weigh_y(h):
+            yw[h] = tile([P, PACK, HALF], F32, "yw%d" % h)
+            for t in range(PACK):
+                nc.scalar.activation(yw[h][:, t, :], y_raw[h][t // 2][:, t % 2, :], COPY, scale=weights[:, t : t + 1])
+
+        def form_g(h, t, lo=0, hi=HALF):
             nc.vector.scalar_tensor_tensor(
-                g_rows[:, t, lo:hi],
-                scores(1, 0) if (t, lo) == (0, P) else banks[t][:, lo:hi],
-                weights[:, t : t + 1],
-                yw[:, t, lo:hi],
-                MULT,
-                SUB,
+                g_rows[h][:, t, lo:hi], scores[h, t][:, lo:hi], weights[:, t : t + 1], yw[h][:, t, lo:hi], MULT, SUB
             )
 
         def interleave(copy, woven, rows):
             copy(woven.rearrange("p (c i) t -> p c t i", i=4), rows.rearrange("p t (c i) -> p c t i", i=4))
 
-        def quantise_g(h):
-            cols = slice((h + 1) * HALF, (h + 2) * HALF)
+        def quantise_g(h, lo=0, hi=HALF):
+            cols = slice(h * HALF + lo, h * HALF + hi)
             nc.vector.quantize_mx(
                 out=g_codes[:, cols].bitcast(E5M2),
                 scales=g_scale[:, cols],
-                in_=g_bf[h][:].rearrange("p i t -> p (i t)"),
+                in_=g_bf[h][:, lo:hi, :].rearrange("p i t -> p (i t)"),
             )
 
-        def round_xm(first, last, tag):
-            rounded = keep.tile([P, (last - first) * P, PACK], BF16, name="xm_bf%d" % first, tag=tag, align_bytes=64)
+        def round_xm(engine, first, last):
+            rounded = tile([P, (last - first) * P, PACK], BF16, "xm_bf%d" % first)
             for b in range(first, last):
-                c = [lo <= b * P < hi for lo, hi in XM_CHUNKS].index(True)
-                lo = b * P - XM_CHUNKS[c][0]
-                nc.scalar.copy(
-                    rounded[:, (b - first) * P : (b - first + 1) * P, :].rearrange("p (c i) t -> p c t i", i=4),
-                    xm_raw[c][:, :, lo : lo + P].rearrange("p t (c i) -> p c t i", i=4),
-                )
-            return rounded
+                c = [lo <= b < hi for lo, hi in XM_LOADS].index(True)
+                lo = (b - XM_LOADS[c][0]) * P
+                woven, rows = rounded[:, (b - first) * P : (b - first + 1) * P, :], xm_raw[c][:, :, lo : lo + P]
+                if engine is nc.gpsimd:
+                    engine.tensor_copy(woven, rows.rearrange("p t d -> p d t"))
+                else:
+                    interleave(nc.scalar.copy if engine is nc.scalar else engine.tensor_copy, woven, rows)
+            return rounded[:]
 
         def quantise_xm(first, last, rounded):
-            cols = slice(first * P, last * P)
+            codes = tile([P, (last - first) * P], U32, "xm_codes%d" % first)
+            for b in range(first, last):
+                xm_codes[b] = codes[:, (b - first) * P : (b - first + 1) * P]
             nc.vector.quantize_mx(
-                out=xm_codes[:, cols].bitcast(E4M3),
-                scales=xm_scale[:, cols],
+                out=codes[:].bitcast(E4M3),
+                scales=xm_scale[:, first * P : last * P],
                 in_=rounded.rearrange("p d t -> p (d t)"),
             )
 
-        products = []
+        ones = tile([P, 1], F32, "ones")
+        nc.vector.memset(ones[:], 1.0)
+        sums = {}
+        pieces = {}
 
-        def multiply(b, start, lo, hi, piece):
-            acc = psum.tile([P, N], F32, name="acc", tag=PRODUCT_BANKS[len(products) % PACK])
-            products.append(b)
+        def multiply(b, lo, hi, bank):
+            sums[b, lo] = psum.tile([P, hi - lo], F32, name="acc", tag="bank%d" % bank)
             nc.tensor.matmul_mx(
-                out=acc[:],
-                lhsT=xm_codes[:, b * P : (b + 1) * P].bitcast(E4M3),
+                out=sums[b, lo][:],
+                lhsT=xm_codes[b].bitcast(E4M3),
                 lhsT_scale=xm_scale[:, b * P : (b + 1) * P],
-                rhs=g_codes[:, start : start + N].bitcast(E5M2),
-                rhs_scale=g_scale[:, start : start + N],
+                rhs=g_codes[:, lo:hi].bitcast(E5M2),
+                rhs_scale=g_scale[:, lo:hi],
                 start=True,
                 stop=True,
             )
-            nc.scalar.copy(piece[:], acc[:, lo:hi])
 
-        def scatter(b, lo, hi, piece):
-            nc.vector.tensor_copy(windows[b % WINDOWS][:].indirect(offsets[:, lo // 16 : hi // 16]), piece[:])
+        def on_scalar(b, lo):
+            return b % 2 == 1 or (b == 0 and lo < HALF)
 
-        def store(b):
-            nc.sync.dma_start(out[b * P : (b + 1) * P, :], windows[b % WINDOWS][:])
+        def empty(b, lo, hi):
+            first = lo // HALF * HALF if b == 0 else 0
+            if lo == first:
+                pieces[b, lo] = tile([P, HALF if b == 0 else N], F32, "piece%d_%d" % (b, lo))
+            copy = nc.scalar.copy if on_scalar(b, lo) else nc.vector.tensor_copy
+            copy(pieces[b, first][:, lo - first : hi - first], sums[b, lo][:])
 
-        dense = {}
-
-        def multiply_whole(b):
-            dense[b] = ring.tile([P, N], F32, name="whole", tag="dense", align_bytes=64)
-            multiply(b, HALF, 0, N, dense[b])
-
-        def multiply_half(b, h, tag):
-            piece = keep.tile([P, HALF], F32, name="half%d%d" % (b, h), tag=tag, align_bytes=64)
-            multiply(b, h * HALF, HALF, N, piece)
-            return piece
-
-        for t in range(PACK):
-            nc.scalar.activation(yw[:, t, :], y_raw[0][t // 2][:, t % 2, :], COPY, scale=weights[:, t : t + 1])
-        rounded0 = round_xm(0, 1, "xm_bf0")
-        for t in range(PACK):
-            if 0 < t < PACK - 1:
-                form_g(t)
+        def scatter(b, lo, hi):
+            places = windows[b % WINDOWS][:].indirect(offsets[:, lo // 16 : hi // 16])
+            if on_scalar(b, lo):
+                nc.scalar.activation(places, pieces[b, lo][:], COPY, scale=ones[:])
             else:
-                form_g(t, 0, P)
-                form_g(t, P, HALF)
+                nc.vector.tensor_copy(places, pieces[b, lo][:])
+            if hi == N:
+                nc.sync.dma_start(out[b * P : (b + 1) * P, :], windows[b % WINDOWS][:])
+
+        weigh_y(0)
+        rounded0 = round_xm(nc.scalar, 0, 1)
+        quarters = ((0, P), (P, HALF))
         for t in range(PACK):
-            for q in range(2, 4):
-                for o in range(PASSES):
-                    score_pass(o, q, t)
-        for copy, lo, hi in (
-            (nc.scalar.copy, VECTOR_SLOTS, HALF),
-            (nc.vector.tensor_copy, 0, P),
-            (nc.vector.tensor_copy, P, VECTOR_SLOTS),
-        ):
-            interleave(copy, g_bf[0][:, lo:hi, :], g_rows[:, :, lo:hi])
-        rounded1 = round_xm(1, 2, "g_rows")
-        quantise_xm(0, 1, rounded0[:])
-        quantise_g(0)
-        half00 = multiply_half(0, 0, "half00")
-        for lo, hi in ((0, SCALAR_SLOTS), (SCALAR_SLOTS, HALF)):
-            for u in range(2):
-                nc.vector.tensor_tensor(
-                    residual[:, 2 * u : 2 * u + 2, lo:hi], pairs[u][:, :, lo:hi], y_raw[1][u][:, :, lo:hi], SUB
-                )
-            if lo == 0:
-                quantise_xm(1, 2, rounded1[:])
+            form_g(0, t)
         for t in range(PACK):
-            nc.scalar.activation(late_rows[:, t, :], residual[:, t, :SCALAR_SLOTS], COPY, scale=weights[:, t : t + 1])
-        interleave(nc.scalar.copy, g_bf[1][:, :SCALAR_SLOTS, :], late_rows[:])
-        nc.gpsimd.tensor_tensor(
-            g_bf[1][:, SCALAR_SLOTS:, :],
-            residual[:, :, SCALAR_SLOTS:].rearrange("p t i -> p i t"),
-            weights[:].unsqueeze(1).to_broadcast([P, HALF - SCALAR_SLOTS, PACK]),
-            MULT,
-        )
-        half10 = multiply_half(1, 0, "residual")
-        scatter(0, 0, HALF, half00)
-        quantise_g(1)
-        rounded23 = round_xm(2, 4, "g_bf1")
-        half01 = multiply_half(0, 1, "half01")
-        half11 = multiply_half(1, 1, "half11")
-        quantise_xm(2, 4, rounded23[:])
-        windows.append(keep.tile([P, T], F32, name="window2", tag="g_bf1", align_bytes=64))
-        nc.gpsimd.memset(windows[2][:].bitcast(I32), 0)
-        scatter(1, 0, HALF, half10)
-        scatter(0, HALF, N, half01)
-        store(0)
-        late = round_xm(4, 8, "xm_raw384")
-        multiply_whole(2)
-        scatter(1, HALF, N, half11)
-        store(1)
-        quantise_xm(4, 6, late[:, : 2 * P, :])
-        quantise_xm(6, 8, late[:, 2 * P :, :])
+            for o in range(PASSES):
+                score(o, 1, t)
+        for lo, hi in quarters:
+            interleave(nc.vector.tensor_copy, g_bf[0][:, lo:hi, :], g_rows[0][:, :, lo:hi])
+        quantise_xm(0, 1, rounded0)
+        for bank, (lo, hi) in zip((5, 4), quarters):
+            quantise_g(0, lo, hi)
+            multiply(0, lo, hi, bank)
+        weigh_y(1)
+        rounded1 = round_xm(nc.scalar, 1, 2)
+        for lo, hi in quarters:
+            empty(0, lo, hi)
+        rounded2 = round_xm(nc.scalar, 2, 3)
+        scatter(0, 0, HALF)
+        for t in range(PACK - 1):
+            form_g(1, t)
+        for lo, hi in quarters:
+            form_g(1, PACK - 1, lo, hi)
+        for lo, hi in quarters:
+            interleave(nc.vector.tensor_copy, g_bf[1][:, lo:hi, :], g_rows[1][:, :, lo:hi])
+        quantise_xm(1, 2, rounded1)
+        multiply(1, 0, HALF, 4)
+        for bank, (lo, hi) in zip((7, 5), quarters):
+            quantise_g(1, lo, hi)
+            multiply(0, HALF + lo, HALF + hi, bank)
+        multiply(1, HALF, N, 6)
+        quantise_xm(2, 3, rounded2)
+        rounded3 = round_xm(nc.vector, 3, 4)
+        for lo, hi in quarters:
+            empty(0, HALF + lo, HALF + hi)
+        quantise_xm(3, 4, rounded3)
+        scatter(0, HALF, N)
+        empty(1, 0, HALF)
+        empty(1, HALF, N)
+        scatter(1, 0, N)
         for b in range(2, BLOCKS):
-            if b + 1 < BLOCKS:
-                multiply_whole(b + 1)
-            scatter(b, 0, N, dense[b])
-            store(b)
+            if b <= 4:
+                multiply(b, 0, N, 5 + b % 2)
+            empty(b, 0, N)
+            if b == 2:
+                quantise_xm(4, 5, round_xm(nc.gpsimd, 4, 5))
+            if b == 4:
+                quantise_xm(5, 8, round_xm(nc.gpsimd, 5, 8))
+                for later in (5, 7, 6):
+                    multiply(later, 0, N, later - 5)
+            scatter(b, 0, N)

@@ -54,8 +54,8 @@ def tile_attend_gsq_w_kernel(tc, xT, w_words, w_scales, y, wt, xm, offs, out):
 
         def tile(shape, dtype, name, tag=None):
             if name in PLACES:
-                return shared.tile(shape, dtype, name=name, align_bytes=64, offset=PLACES[name])
-            return keep.tile(shape, dtype, name=name, tag=tag or name, align_bytes=64)
+                return shared.tile(shape, dtype, name=name, align_bytes=256, offset=PLACES[name])
+            return keep.tile(shape, dtype, name=name, tag=tag or name, align_bytes=256)
 
         offsets = keep.tile([P, N // 16], U16, name="offsets")
         word_table = tile([P, T], I32, "word_table")

@@ -24,8 +24,8 @@ PASSES = D // (P * PACK)
 BLOCKS = D // P
 HALF = N // 2
 WINDOWS = 4
-XT_LOADS = ((0, 0, R), (1, 0, R // 2), (1, R // 2, R))
-VECTOR_M = ((0, 0), (0, 0), (64, 12))
+XT_LOADS = tuple((o, lo, lo + R // 2) for o in range(PASSES) for lo in (0, R // 2))
+VECTOR_M = ((0, 0), (0, 0), (0, 0), (64, 16))
 PLACES = {
     "window3": 0,
     "scale_table": 0,
@@ -38,11 +38,13 @@ PLACES = {
     "xm_bf5": 8192,
     "piece4_0": 12288,
     "piece6_0": 12288,
+    "yw02": 16384,
+    "xm_codes0": 16384,
     "xm_raw2": 14336,
     "piece0_0": 14336,
 }
-WORDS_FIRST = 768
-XM_LOADS = tuple((b, b + 1) for b in range(BLOCKS))
+XM_LOADS = ((0, 1), (1, 2), (2, 3), (3, 4), (4, 5), (5, 6), (6, 8))
+Y_LOADS = (((0, 1), (1, 2), (2, 4)), ((0, 2), (2, 4)))
 
 
 def tile_attend_gsq_w_kernel(tc, xT, w_words, w_scales, y, wt, xm, offs, out):
@@ -63,11 +65,11 @@ def tile_attend_gsq_w_kernel(tc, xT, w_words, w_scales, y, wt, xm, offs, out):
         w_scale = tile([P, PASSES, N], U8, "w_scale")
         weights = tile([P, PACK], F32, "weights")
         xt_raw = [tile([P, PACK, hi - lo], F32, "xt_raw%d_%d" % (o, lo)) for o, lo, hi in XT_LOADS]
-        y_raw = [[tile([P, 2, HALF], F32, "y_raw%d%d" % (h, u)) for u in range(2)] for h in range(2)]
+        y_raw = [[tile([P, hi - lo, HALF], F32, "y_raw%d%d" % (h, lo)) for lo, hi in Y_LOADS[h]] for h in range(2)]
         xm_raw = [tile([P, PACK, (hi - lo) * P], F32, "xm_raw%d" % lo) for lo, hi in XM_LOADS]
         windows = [tile([P, T], F32, "window%d" % w) for w in range(WINDOWS - 1)]
 
-        nc.vector.memset(scale_table[:].bitcast(I32), 0)
+        nc.gpsimd.memset(scale_table[:].bitcast(I32), 0)
 
         xt_rows = [xT[0, 512 * o : 512 * (o + 1), :].rearrange("(p j) r -> p j r", j=PACK) for o in range(PASSES)]
 
@@ -75,15 +77,14 @@ def tile_attend_gsq_w_kernel(tc, xT, w_words, w_scales, y, wt, xm, offs, out):
             o, lo, hi = XT_LOADS[k]
             nc.sync.dma_start(xt_raw[k][:], xt_rows[o][:, :, lo:hi])
 
-        word_rows = w_words[0].rearrange("p t b -> p (t b)").bitcast(I32)
-        nc.sync.dma_start(word_table[:, :WORDS_FIRST], word_rows[:, :WORDS_FIRST])
+        load_xt(0)
         nc.sync.dma_start(offsets[:], offs)
         nc.sync.dma_start(scale_table[0:P:4, :].bitcast(I32), w_scales.bitcast(I32).rearrange("o f w -> f o w"))
-        load_xt(0)
-        nc.sync.dma_start(word_table[:, WORDS_FIRST:], word_rows[:, WORDS_FIRST:])
+        nc.sync.dma_start(word_table[:], w_words[0].rearrange("p t b -> p (t b)").bitcast(I32))
+        load_xt(1)
 
         planes = w_scale[:].rearrange("p o i -> p (o i)").bitcast(I32)
-        nc.vector.memset(planes, 0)
+        nc.gpsimd.memset(planes, 0)
         for window in windows:
             nc.vector.memset(window[:].bitcast(I32), 0)
 
@@ -97,14 +98,14 @@ def tile_attend_gsq_w_kernel(tc, xT, w_words, w_scales, y, wt, xm, offs, out):
         xm_rows = xm[0].rearrange("(p t) d -> p t d", t=PACK)
 
         def load_y(h):
-            for u in range(2):
-                nc.sync.dma_start(y_raw[h][u][:], y_rows[:, 2 * u : 2 * u + 2, h * HALF : (h + 1) * HALF])
+            for k, (lo, hi) in enumerate(Y_LOADS[h]):
+                nc.sync.dma_start(y_raw[h][k][:], y_rows[:, lo:hi, h * HALF : (h + 1) * HALF])
 
-        load_xt(1)
-        for q in range(0, P, 32):
-            nc.sync.dma_start(planes[q : q + 4, :], scale_rows[q : q + 32 : 4, :].bitcast(I32))
-        load_xt(2)
         nc.sync.dma_start(weights[:], wt[0].rearrange("(p t) one -> p (t one)", t=PACK))
+        load_xt(2)
+        for q in (0, 64, 32, 96):
+            nc.sync.dma_start(planes[q : q + 4, :], scale_rows[q : q + 32 : 4, :].bitcast(I32))
+        load_xt(3)
         for c, (lo, hi) in enumerate(XM_LOADS):
             if c < 2:
                 load_y(c)
@@ -153,17 +154,15 @@ def tile_attend_gsq_w_kernel(tc, xT, w_words, w_scales, y, wt, xm, offs, out):
             by_pass = pair_words[:, h * HALF : (h + 1) * HALF].bitcast(U16).rearrange("p (i o) -> p o i", o=PASSES)
             nc.vector.tensor_copy(w_codes[h][:].bitcast(U16), by_pass)
 
-        round_xt(0)
-        for t in range(2):
-            quantise_xt(0, t)
         nc.vector.tensor_copy(pair_words[:], word_table[:].bitcast(U32).indirect(offsets[:]))
         split(0)
-        for t in range(PACK):
-            if t >= 2:
-                quantise_xt(0, t)
-            score(0, 0, t)
+        round_xt(0)
         round_xt(1)
+        for t in range(PACK):
+            quantise_xt(0, t)
+            score(0, 0, t)
         round_xt(2)
+        round_xt(3)
         for t in range(PACK):
             quantise_xt(1, t)
             score(1, 0, t)
@@ -178,13 +177,14 @@ def tile_attend_gsq_w_kernel(tc, xT, w_words, w_scales, y, wt, xm, offs, out):
         xm_scale = tile([P, D], U8, "xm_scale")
 
         def weigh_y(h):
-            yw[h] = tile([P, PACK, HALF], F32, "yw%d" % h)
-            for t in range(PACK):
-                nc.scalar.activation(yw[h][:, t, :], y_raw[h][t // 2][:, t % 2, :], COPY, scale=weights[:, t : t + 1])
+            for k, (lo, hi) in enumerate(Y_LOADS[h]):
+                for t in range(lo, hi):
+                    yw[h, t] = tile([P, HALF], F32, "yw%d%d" % (h, t))
+                    nc.scalar.activation(yw[h, t][:], y_raw[h][k][:, t - lo, :], COPY, scale=weights[:, t : t + 1])
 
         def form_g(h, t, lo=0, hi=HALF):
             nc.vector.scalar_tensor_tensor(
-                g_rows[h][:, t, lo:hi], scores[h, t][:, lo:hi], weights[:, t : t + 1], yw[h][:, t, lo:hi], MULT, SUB
+                g_rows[h][:, t, lo:hi], scores[h, t][:, lo:hi], weights[:, t : t + 1], yw[h, t][:, lo:hi], MULT, SUB
             )
 
         def interleave(copy, woven, rows):
@@ -221,7 +221,7 @@ def tile_attend_gsq_w_kernel(tc, xT, w_words, w_scales, y, wt, xm, offs, out):
             )
 
         ones = tile([P, 1], F32, "ones")
-        nc.vector.memset(ones[:], 1.0)
+        nc.gpsimd.memset(ones[:], 1.0)
         sums = {}
         pieces = {}
 

from contextlib import ExitStack

import concourse.mybir as mybir

D, T, R, N = 1024, 2048, 512, 512
FLOPS = 2 * 2 * R * N * D

F32 = mybir.dt.float32
BF16 = mybir.dt.bfloat16
I32 = mybir.dt.int32
U32 = mybir.dt.uint32
U16 = mybir.dt.uint16
U8 = mybir.dt.uint8
E4M3 = mybir.dt.float8_e4m3fn_x4
E5M2 = mybir.dt.float8_e5m2_x4
E2M1 = mybir.dt.float4_e2m1fn_x4
COPY = mybir.ActivationFunctionType.Copy
MULT = mybir.AluOpType.mult
SUB = mybir.AluOpType.subtract

P = 128
PACK = 4
PASSES = D // (P * PACK)
BLOCKS = D // P
HALF = N // 2
WINDOWS = 4
XT_LOADS = tuple((o, lo, lo + R // 2) for o in range(PASSES) for lo in (0, R // 2))
VECTOR_M = ((0, 0), (0, 0), (0, 0), (64, 16))
PLACES = {
    "window3": 0,
    "scale_table": 0,
    "xt_bf11": 18432,
    "w_codes1": 18432,
    "g_bf1": 8192,
    "xm_bf3": 8192,
    "xm_codes2": 9216,
    "xm_bf4": 8192,
    "xm_bf5": 8192,
    "piece4_0": 12288,
    "piece6_0": 12288,
    "yw02": 16384,
    "xm_codes0": 16384,
    "xm_raw2": 14336,
    "piece0_0": 14336,
}
XM_LOADS = ((0, 1), (1, 2), (2, 3), (3, 4), (4, 5), (5, 6), (6, 8))
Y_LOADS = (((0, 1), (1, 2), (2, 4)), ((0, 2), (2, 4)))


def tile_attend_gsq_w_kernel(tc, xT, w_words, w_scales, y, wt, xm, offs, out):
    nc = tc.nc
    with ExitStack() as ctx:
        keep = ctx.enter_context(tc.tile_pool(name="keep", bufs=1))
        shared = ctx.enter_context(tc.tile_pool(name="shared", bufs=1))
        psum = ctx.enter_context(tc.psum_pool(name="psum", bufs=1))

        def tile(shape, dtype, name, tag=None):
            if name in PLACES:
                return shared.tile(shape, dtype, name=name, align_bytes=256, offset=PLACES[name])
            return keep.tile(shape, dtype, name=name, tag=tag or name, align_bytes=256)

        offsets = keep.tile([P, N // 16], U16, name="offsets")
        word_table = tile([P, T], I32, "word_table")
        scale_table = tile([P, T], U8, "scale_table")
        w_scale = tile([P, PASSES, N], U8, "w_scale")
        weights = tile([P, PACK], F32, "weights")
        xt_raw = [tile([P, PACK, hi - lo], F32, "xt_raw%d_%d" % (o, lo)) for o, lo, hi in XT_LOADS]
        y_raw = [[tile([P, hi - lo, HALF], F32, "y_raw%d%d" % (h, lo)) for lo, hi in Y_LOADS[h]] for h in range(2)]
        xm_raw = [tile([P, PACK, (hi - lo) * P], F32, "xm_raw%d" % lo) for lo, hi in XM_LOADS]
        windows = [tile([P, T], F32, "window%d" % w) for w in range(WINDOWS - 1)]

        nc.gpsimd.memset(scale_table[:].bitcast(I32), 0)

        xt_rows = [xT[0, 512 * o : 512 * (o + 1), :].rearrange("(p j) r -> p j r", j=PACK) for o in range(PASSES)]

        def load_xt(k):
            o, lo, hi = XT_LOADS[k]
            nc.sync.dma_start(xt_raw[k][:], xt_rows[o][:, :, lo:hi])

        load_xt(0)
        nc.sync.dma_start(offsets[:], offs)
        nc.sync.dma_start(scale_table[0:P:4, :].bitcast(I32), w_scales.bitcast(I32).rearrange("o f w -> f o w"))
        nc.sync.dma_start(word_table[:], w_words[0].rearrange("p t b -> p (t b)").bitcast(I32))
        load_xt(1)

        planes = w_scale[:].rearrange("p o i -> p (o i)").bitcast(I32)
        nc.gpsimd.memset(planes, 0)
        for window in windows:
            nc.vector.memset(window[:].bitcast(I32), 0)

        scale_rows = tile([P, N], U8, "scale_rows")
        nc.vector.tensor_copy(scale_rows[:], scale_table[:].indirect(offsets[:]))
        windows.append(tile([P, T], F32, "window3"))
        for window in windows[3:]:
            nc.vector.memset(window[:].bitcast(I32), 0)

        y_rows = y[0].rearrange("(p t) i -> p t i", t=PACK)
        xm_rows = xm[0].rearrange("(p t) d -> p t d", t=PACK)

        def load_y(h):
            for k, (lo, hi) in enumerate(Y_LOADS[h]):
                nc.sync.dma_start(y_raw[h][k][:], y_rows[:, lo:hi, h * HALF : (h + 1) * HALF])

        nc.sync.dma_start(weights[:], wt[0].rearrange("(p t) one -> p (t one)", t=PACK))
        load_xt(2)
        for q in (0, 64, 32, 96):
            nc.sync.dma_start(planes[q : q + 4, :], scale_rows[q : q + 32 : 4, :].bitcast(I32))
        load_xt(3)
        for c, (lo, hi) in enumerate(XM_LOADS):
            if c < 2:
                load_y(c)
            nc.sync.dma_start(xm_raw[c][:], xm_rows[:, :, lo * P : hi * P])

        pair_words = tile([P, N], U32, "pair_words")
        w_codes = {}
        xt_codes = tile([P, PASSES, R], U32, "xt_codes")
        xt_scale = tile([P, PASSES, R], U8, "xt_scale")
        xt_bf = [[tile([P, 2, P, PACK], BF16, "xt_bf%d%d" % (o, u)) for u in range(2)] for o in range(PASSES)]
        scores = {}

        def round_xt(k):
            o, lo, hi = XT_LOADS[k]
            src = xt_raw[k][:].rearrange("p j (m t) -> p m j t", t=PACK)
            for u in range(2):
                dst = xt_bf[o][u][:].rearrange("p t m j -> p m j t")[:, lo // PACK : hi // PACK, :, :]
                mv = VECTOR_M[k][u]
                if mv < (hi - lo) // PACK:
                    nc.scalar.copy(dst[:, mv:, :, :], src[:, mv:, :, 2 * u : 2 * u + 2])
                if mv:
                    nc.vector.tensor_copy(dst[:, :mv, :, :], src[:, :mv, :, 2 * u : 2 * u + 2])

        def quantise_xt(o, t):
            nc.vector.quantize_mx(
                out=xt_codes[:, o, P * t : P * (t + 1)].bitcast(E4M3),
                scales=xt_scale[:, o, P * t : P * (t + 1)],
                in_=xt_bf[o][t // 2][:, t % 2, :, :].rearrange("p m j -> p (m j)"),
            )

        def score(o, h, t):
            if o == 0:
                scores[h, t] = psum.tile([P, HALF], F32, name="scores", tag="bank%d" % t)
            nc.tensor.matmul_mx(
                out=scores[h, t][:],
                lhsT=xt_codes[:, o, P * t : P * (t + 1)].bitcast(E4M3),
                lhsT_scale=xt_scale[:, o, P * t : P * (t + 1)],
                rhs=w_codes[h][:, o, :].bitcast(E2M1),
                rhs_scale=w_scale[:, o, HALF * h : HALF * (h + 1)],
                start=(o == 0),
                stop=(o == PASSES - 1),
            )

        def split(h):
            w_codes[h] = tile([P, PASSES, 2 * HALF], U8, "w_codes%d" % h)
            by_pass = pair_words[:, h * HALF : (h + 1) * HALF].bitcast(U16).rearrange("p (i o) -> p o i", o=PASSES)
            nc.vector.tensor_copy(w_codes[h][:].bitcast(U16), by_pass)

        nc.vector.tensor_copy(pair_words[:], word_table[:].bitcast(U32).indirect(offsets[:]))
        split(0)
        round_xt(0)
        round_xt(1)
        for t in range(PACK):
            quantise_xt(0, t)
            score(0, 0, t)
        round_xt(2)
        round_xt(3)
        for t in range(PACK):
            quantise_xt(1, t)
            score(1, 0, t)
        split(1)

        yw = {}
        g_rows = [tile([P, PACK, HALF], BF16, "g_rows%d" % h) for h in range(2)]
        g_bf = [tile([P, HALF, PACK], BF16, "g_bf%d" % h) for h in range(2)]
        g_codes = tile([P, N], U32, "g_codes")
        g_scale = tile([P, N], U8, "g_scale")
        xm_codes = {}
        xm_scale = tile([P, D], U8, "xm_scale")

        def weigh_y(h):
            for k, (lo, hi) in enumerate(Y_LOADS[h]):
                for t in range(lo, hi):
                    yw[h, t] = tile([P, HALF], F32, "yw%d%d" % (h, t))
                    nc.scalar.activation(yw[h, t][:], y_raw[h][k][:, t - lo, :], COPY, scale=weights[:, t : t + 1])

        def form_g(h, t, lo=0, hi=HALF):
            nc.vector.scalar_tensor_tensor(
                g_rows[h][:, t, lo:hi], scores[h, t][:, lo:hi], weights[:, t : t + 1], yw[h, t][:, lo:hi], MULT, SUB
            )

        def interleave(copy, woven, rows):
            copy(woven.rearrange("p (c i) t -> p c t i", i=4), rows.rearrange("p t (c i) -> p c t i", i=4))

        def quantise_g(h, lo=0, hi=HALF):
            cols = slice(h * HALF + lo, h * HALF + hi)
            nc.vector.quantize_mx(
                out=g_codes[:, cols].bitcast(E5M2),
                scales=g_scale[:, cols],
                in_=g_bf[h][:, lo:hi, :].rearrange("p i t -> p (i t)"),
            )

        def round_xm(engine, first, last):
            rounded = tile([P, (last - first) * P, PACK], BF16, "xm_bf%d" % first)
            for b in range(first, last):
                c = [lo <= b < hi for lo, hi in XM_LOADS].index(True)
                lo = (b - XM_LOADS[c][0]) * P
                woven, rows = rounded[:, (b - first) * P : (b - first + 1) * P, :], xm_raw[c][:, :, lo : lo + P]
                if engine is nc.gpsimd:
                    engine.tensor_copy(woven, rows.rearrange("p t d -> p d t"))
                else:
                    interleave(nc.scalar.copy if engine is nc.scalar else engine.tensor_copy, woven, rows)
            return rounded[:]

        def quantise_xm(first, last, rounded):
            codes = tile([P, (last - first) * P], U32, "xm_codes%d" % first)
            for b in range(first, last):
                xm_codes[b] = codes[:, (b - first) * P : (b - first + 1) * P]
            nc.vector.quantize_mx(
                out=codes[:].bitcast(E4M3),
                scales=xm_scale[:, first * P : last * P],
                in_=rounded.rearrange("p d t -> p (d t)"),
            )

        ones = tile([P, 1], F32, "ones")
        nc.gpsimd.memset(ones[:], 1.0)
        sums = {}
        pieces = {}

        def multiply(b, lo, hi, bank):
            sums[b, lo] = psum.tile([P, hi - lo], F32, name="acc", tag="bank%d" % bank)
            nc.tensor.matmul_mx(
                out=sums[b, lo][:],
                lhsT=xm_codes[b].bitcast(E4M3),
                lhsT_scale=xm_scale[:, b * P : (b + 1) * P],
                rhs=g_codes[:, lo:hi].bitcast(E5M2),
                rhs_scale=g_scale[:, lo:hi],
                start=True,
                stop=True,
            )

        def on_scalar(b, lo):
            return b % 2 == 1 or (b == 0 and lo < HALF)

        def empty(b, lo, hi):
            first = lo // HALF * HALF if b == 0 else 0
            if lo == first:
                pieces[b, lo] = tile([P, HALF if b == 0 else N], F32, "piece%d_%d" % (b, lo))
            copy = nc.scalar.copy if on_scalar(b, lo) else nc.vector.tensor_copy
            copy(pieces[b, first][:, lo - first : hi - first], sums[b, lo][:])

        def scatter(b, lo, hi):
            places = windows[b % WINDOWS][:].indirect(offsets[:, lo // 16 : hi // 16])
            if on_scalar(b, lo):
                nc.scalar.activation(places, pieces[b, lo][:], COPY, scale=ones[:])
            else:
                nc.vector.tensor_copy(places, pieces[b, lo][:])
            if hi == N:
                nc.sync.dma_start(out[b * P : (b + 1) * P, :], windows[b % WINDOWS][:])

        weigh_y(0)
        rounded0 = round_xm(nc.scalar, 0, 1)
        quarters = ((0, P), (P, HALF))
        for t in range(PACK):
            form_g(0, t)
        for t in range(PACK):
            for o in range(PASSES):
                score(o, 1, t)
        for lo, hi in quarters:
            interleave(nc.vector.tensor_copy, g_bf[0][:, lo:hi, :], g_rows[0][:, :, lo:hi])
        quantise_xm(0, 1, rounded0)
        for bank, (lo, hi) in zip((5, 4), quarters):
            quantise_g(0, lo, hi)
            multiply(0, lo, hi, bank)
        weigh_y(1)
        rounded1 = round_xm(nc.scalar, 1, 2)
        for lo, hi in quarters:
            empty(0, lo, hi)
        rounded2 = round_xm(nc.scalar, 2, 3)
        scatter(0, 0, HALF)
        for t in range(PACK - 1):
            form_g(1, t)
        for lo, hi in quarters:
            form_g(1, PACK - 1, lo, hi)
        for lo, hi in quarters:
            interleave(nc.vector.tensor_copy, g_bf[1][:, lo:hi, :], g_rows[1][:, :, lo:hi])
        quantise_xm(1, 2, rounded1)
        multiply(1, 0, HALF, 4)
        for bank, (lo, hi) in zip((7, 5), quarters):
            quantise_g(1, lo, hi)
            multiply(0, HALF + lo, HALF + hi, bank)
        multiply(1, HALF, N, 6)
        quantise_xm(2, 3, rounded2)
        rounded3 = round_xm(nc.vector, 3, 4)
        for lo, hi in quarters:
            empty(0, HALF + lo, HALF + hi)
        quantise_xm(3, 4, rounded3)
        scatter(0, HALF, N)
        empty(1, 0, HALF)
        empty(1, HALF, N)
        scatter(1, 0, N)
        for b in range(2, BLOCKS):
            if b <= 4:
                multiply(b, 0, N, 5 + b % 2)
            empty(b, 0, N)
            if b == 2:
                quantise_xm(4, 5, round_xm(nc.gpsimd, 4, 5))
            if b == 4:
                quantise_xm(5, 8, round_xm(nc.gpsimd, 5, 8))
                for later in (5, 7, 6):
                    multiply(later, 0, N, later - 5)
            scatter(b, 0, N)
